import numpy as np
import ml_dtypes


def mxq(x, axis, fmt="e4m3"):
    dtype, down = {"e4m3": (ml_dtypes.float8_e4m3fn, 7), "e5m2": (ml_dtypes.float8_e5m2, 14)}[fmt]
    v = np.moveaxis(np.asarray(x, np.float32).astype(ml_dtypes.bfloat16).astype(np.float64), axis, -1)
    blocks = v.reshape(v.shape[:-1] + (-1, 32))
    amax = np.abs(blocks).max(-1, keepdims=True)
    byte = np.maximum(np.where(amax > 0, np.frexp(amax)[1] - 1 + 127, 0) - down, 1)
    scale = np.exp2(byte - 127.0)
    codes = (blocks / scale).astype(np.float32).astype(dtype).astype(np.float64)
    return np.moveaxis((codes * scale).reshape(v.shape), -1, axis)


WIDE = False


def mx_kscale(k):
    if not WIDE:
        return np.ones(k)
    levels = np.array([10, -10, 5, -5, 0])
    if k % 512:
        return np.exp2(np.random.permutation(np.resize(levels, k // 32))).repeat(32)
    a = np.empty((k // 512, 16))
    for p in range(k // 512):
        a[p, :8] = np.random.permutation(np.resize(levels, 8))
        for g in range(8):
            far = levels[np.abs(levels - a[p, g]) >= 10]
            a[p, g + 8] = far[np.random.randint(len(far))]
    return np.exp2(a.ravel()).repeat(32)


def f64(x):
    return np.asarray(x).astype(np.float64)


def striped(idx):
    return np.tile(idx.reshape(-1, 16).T, (8, 1)).astype(np.uint16)


def unstriped(offs):
    return offs[:16].T.reshape(-1).astype(np.int64)


E2M1 = np.array([0.0, 0.5, 1.0, 1.5, 2.0, 3.0, 4.0, 6.0, -0.0, -0.5, -1.0, -1.5, -2.0, -3.0, -4.0, -6.0])


def pack_weight(w, fmt):
    k, n = w.shape
    w = f64(np.asarray(w, np.float32).astype(ml_dtypes.bfloat16)).reshape(k // 32, 32, n)
    amax = np.abs(w).max(1)
    if fmt == "e4m3":
        byte = np.frexp(amax)[1] - 1 + 127 - 7
    else:
        mant, ex = np.frexp(amax / 6.0)
        byte = np.where(mant > 0.5, ex, ex - 1) + 127
    byte = np.clip(np.where(amax > 0, byte, 1), 1, 254)
    scaled = (w * np.exp2(127.0 - byte)[:, None, :]).reshape(k, n).astype(np.float32)
    by_word = np.ascontiguousarray(scaled.reshape(k // 512, 128, 4, n).transpose(0, 1, 3, 2))
    if fmt == "e4m3":
        words = by_word.astype(ml_dtypes.float8_e4m3fn).view(np.uint8)
    else:
        c = by_word.astype(ml_dtypes.float4_e2m1fn).view(np.uint8) & 0xF
        words = (c[..., 0::2] | (c[..., 1::2] << 4)).reshape(k // 512, 128, 2 * n)
    return np.ascontiguousarray(words), np.ascontiguousarray(byte.astype(np.uint8).reshape(k // 512, 16, n))


def unpack_weight(words, scales, fmt):
    g, _, n = scales.shape
    words = np.ascontiguousarray(words).reshape(g, 128, n, -1)
    if fmt == "e4m3":
        vals = words.view(ml_dtypes.float8_e4m3fn).astype(np.float64)
    else:
        nib = np.empty((g, 128, n, 4), np.uint8)
        nib[..., 0::2] = words & 0xF
        nib[..., 1::2] = words >> 4
        vals = E2M1[nib]
    vals = vals * np.repeat(np.exp2(scales.astype(np.float64) - 127.0), 8, axis=1)[..., None]
    return vals.transpose(0, 1, 3, 2).reshape(g * 512, n)


def gelu(v):
    return 0.5 * v * (1.0 + np.tanh(np.sqrt(2.0 / np.pi) * (v + 0.044715 * v**3)))


def bf(x):
    return np.asarray(x, np.float32).astype(ml_dtypes.bfloat16)


def planes(Y):
    n, m = Y.shape
    b = f64(bf(Y)).reshape(n // 32, 32, m)
    amax = np.abs(b).max(1)
    byte = np.clip(np.where(amax > 0, np.frexp(amax)[1] - 1 + 127 - 7, 1), 1, 254)
    codes = (b * np.exp2(127.0 - byte)[:, None, :]).reshape(n, m).astype(np.float32).astype(ml_dtypes.float8_e4m3fn).view(np.uint8)
    words = codes.reshape(n // 512, 128, 4, m).transpose(0, 1, 3, 2)
    return np.ascontiguousarray(words), np.ascontiguousarray(byte.astype(np.uint8).reshape(n // 512, 16, m))


K, T, S, H, N = 1024, 4096, 1024, 512, 384


def setup_inputs():
    n = np.random.standard_normal
    s = mx_kscale(K)[:, None]
    u = mx_kscale(H)[:, None]
    tab_words, tab_scales = pack_weight(n((K, T)) * s, "e4m3")
    w2_words, w2_scales = pack_weight(n((K, H)) / s * u.T / np.sqrt(K), "e2m1")
    w3_words, w3_scales = pack_weight(n((K, N)) / s / np.sqrt(K), "e4m3")
    return {
        "tab_words": tab_words, "tab_scales": tab_scales,
        "offs": striped(np.random.permutation(T)[:S]),
        "w1": (n((K, H)) / s / np.sqrt(K)).astype(np.float32),
        "gain": (np.random.uniform(0.4, 0.9, H) * u[:, 0]).astype(np.float32),
        "w2_words": w2_words, "w2_scales": w2_scales,
        "w3_words": w3_words, "w3_scales": w3_scales,
        "w4": (n((H, N)) / u / np.sqrt(H)).astype(np.float32),
    }


def reference(tab_words, tab_scales, offs, w1, gain, w2_words, w2_scales, w3_words, w3_scales, w4):
    v = unpack_weight(tab_words, tab_scales, "e4m3")[:, unstriped(offs)]
    w2 = unpack_weight(w2_words, w2_scales, "e2m1")
    w3 = unpack_weight(w3_words, w3_scales, "e4m3")
    a = mxq(f64(w1), 0, "e4m3").T @ v
    b = w2.T @ v
    h = f64(gain)[:, None] * np.square(a) + b
    words, scales = planes(h)
    q = mxq(f64(w4), 0, "e4m3").T @ mxq(h, 0, "e4m3")
    c = w3.T @ v
    y = c / (1.0 + np.abs(q))
    return y, h, words, scales

@@ -1,0 +1,215 @@
+from contextlib import ExitStack
+
+import concourse.mybir as mybir
+
+K, T, S, H, N = 1024, 4096, 1024, 512, 384
+FLOPS = 2 * S * (2 * K * H + K * N + H * N)
+
+F32 = mybir.dt.float32
+BF16 = mybir.dt.bfloat16
+I32 = mybir.dt.int32
+U32 = mybir.dt.uint32
+U16 = mybir.dt.uint16
+U8 = mybir.dt.uint8
+FP8X4 = mybir.dt.float8_e4m3fn_x4
+FP4X4 = mybir.dt.float4_e2m1fn_x4
+ACT = mybir.ActivationFunctionType
+ALU = mybir.AluOpType
+
+P = 128
+PACK = 4
+PASSES = K // (P * PACK)
+HALF = 512
+HALVES = S // HALF
+NT = N // P
+
+
+def tile_list_speckle_energy_kernel(
+    tc, tab_words, tab_scales, offs, w1, gain, w2_words, w2_scales, w3_words, w3_scales, w4,
+    out_0, out_1, out_2, out_3,
+):
+    nc = tc.nc
+    with ExitStack() as ctx:
+        keep = ctx.enter_context(tc.tile_pool(name="keep", bufs=1))
+        work = ctx.enter_context(tc.tile_pool(name="work", bufs=3))
+        psum = ctx.enter_context(tc.psum_pool(name="psum", bufs=8))
+
+        def held(name, shape, dtype):
+            return keep.tile(shape, dtype, name=name, align_bytes=64)
+
+        offsets = keep.tile([P, S // 16], U16, name="offsets")
+        tab_s = held("tab_s", [P, T], U8)
+        w2_s_raw = held("w2_s_raw", [P, PASSES * H], U8)
+        w3_s = held("w3_s", [P, PASSES * N], U8)
+        v_s1 = held("v_s1", [P, S], U8)
+        one = held("one", [P, 1], F32)
+        warm = held("warm", [P, 1], F32)
+        nc.vector.memset(tab_s[:].bitcast(I32), 0)
+        nc.vector.memset(one[:], 1.0)
+        nc.vector.memset(w2_s_raw[:].bitcast(I32), 0)
+        nc.vector.memset(w3_s[:].bitcast(I32), 0)
+        nc.vector.memset(v_s1[:].bitcast(I32), 0)
+        nc.scalar.activation(warm[:], one[:], ACT.Abs_reciprocal_sqrt)
+
+        w1_raw = [held("w1_raw%d" % a, [P, PACK, H], F32) for a in range(PASSES)]
+        tab_w = [held("tab_w%d" % a, [P, T], U32) for a in range(PASSES)]
+        w2_w_raw = held("w2_w_raw", [P, PASSES, 2 * H], U8)
+        gain_t = held("gain_t", [P, PACK], F32)
+        w1_rows = w1.rearrange("(a p j) c -> a p j c", p=P, j=PACK)
+        nc.sync.dma_start(w1_raw[0][:], w1_rows[0])
+        nc.sync.dma_start(offsets[:], offs)
+        nc.sync.dma_start(gain_t[:], gain.rearrange("(p t) -> p t", t=PACK))
+        nc.sync.dma_start(w1_raw[1][:], w1_rows[1])
+        nc.sync.dma_start(w2_w_raw[:].bitcast(I32), w2_words.rearrange("a p c -> p a c").bitcast(I32))
+        for a in range(PASSES):
+            nc.sync.dma_start(tab_w[a][:].bitcast(I32), tab_words[a].rearrange("p t i -> p (t i)").bitcast(I32))
+        for q in range(4):
+            nc.gpsimd.dma_start(tab_s[32 * q : 32 * q + 8, :].bitcast(I32), tab_scales[:, 4 * q : 4 * q + 4, :].bitcast(I32))
+        for plane, scales in ((w2_s_raw, w2_scales), (w3_s, w3_scales)):
+            for q in range(4):
+                nc.gpsimd.dma_start(
+                    plane[32 * q : 32 * q + 4, :].bitcast(I32).rearrange("r (a c) -> r a c", a=PASSES),
+                    scales[:, 4 * q : 4 * q + 4, :].rearrange("a r c -> r a c").bitcast(I32),
+                )
+
+        w1_w = held("w1_w", [P, PASSES, H], U32)
+        w1_s = held("w1_s", [P, PASSES, H], U8)
+        w1_bf = [held("w1_bf%d" % a, [P, H * PACK], BF16) for a in range(PASSES)]
+        for a in range(PASSES):
+            nc.scalar.copy(
+                w1_bf[a][:].rearrange("p (t m j) -> p m t j", t=PACK, j=PACK),
+                w1_raw[a][:].rearrange("p j (m t) -> p m t j", t=PACK),
+            )
+
+        v_s = held("v_s", [P, S], U8)
+        nc.vector.tensor_copy(v_s[:], tab_s[:].indirect(offsets[:]))
+        for q in range(4):
+            nc.sync.dma_start(v_s1[32 * q : 32 * q + 4, :].bitcast(I32), v_s[32 * q + 4 : 32 * q + 8, :].bitcast(I32))
+        w4_raw = held("w1_raw0", [P, PACK, N], F32)
+        w3_w = held("w1_raw1", [P, PASSES, N], U32)
+        nc.sync.dma_start(w4_raw[:], w4.rearrange("(p j) n -> p j n", j=PACK))
+        nc.sync.dma_start(w3_w[:].bitcast(I32), w3_words.rearrange("a p n i -> p a (n i)").bitcast(I32))
+        v_planes = [v_s, v_s1]
+
+        w2_w = held("w2_w", [P, PASSES, 2 * H], U8)
+        w2_s = held("w2_s", [P, PASSES, H], U8)
+        nc.vector.tensor_copy(
+            w2_w[:].rearrange("p a (t m b) -> p a t m b", t=PACK, b=2),
+            w2_w_raw[:].rearrange("p a (m t b) -> p a t m b", t=PACK, b=2),
+        )
+        nc.vector.quantize_mx(out=w1_w[:, 0, :].bitcast(FP8X4), scales=w1_s[:, 0, :], in_=w1_bf[0][:])
+        nc.vector.quantize_mx(out=w1_w[:, 1, :].bitcast(FP8X4), scales=w1_s[:, 1, :], in_=w1_bf[1][:])
+
+        v_w = [[held("v_w%d%d" % (a, u), [P, HALF], U32) for u in range(HALVES)] for a in range(PASSES)]
+
+        def gather(a, u):
+            cols = HALF // 16
+            nc.vector.tensor_copy(v_w[a][u][:], tab_w[a][:].indirect(offsets[:, u * cols : (u + 1) * cols]))
+
+        gather(0, 0)
+        nc.vector.tensor_copy(
+            w2_s[:].rearrange("p a (t m) -> p a t m", t=PACK),
+            w2_s_raw[:].rearrange("p (a m t) -> p a t m", a=PASSES, t=PACK),
+        )
+        gather(0, 1)
+        gather(1, 0)
+        gather(1, 1)
+
+        w4_bf = held("w4_bf", [P, N * PACK], BF16)
+        w4_w = held("w4_w", [P, N], U32)
+        w4_s = held("w4_s", [P, N], U8)
+        nc.gpsimd.tensor_scalar(
+            w4_bf[:].rearrange("p (c i j) -> p c j i", i=4, j=PACK),
+            w4_raw[:].rearrange("p j (c i) -> p c j i", i=4),
+            1.0, 0.0, ALU.mult, ALU.add,
+        )
+
+        def mm(bank, a, words, scales, u, dtype):
+            nc.tensor.matmul_mx(
+                out=bank[:], lhsT=words.bitcast(dtype), lhsT_scale=scales,
+                rhs=v_w[a][u][:].bitcast(FP8X4), rhs_scale=v_planes[a][:, u * HALF : (u + 1) * HALF],
+                start=(a == 0), stop=(a == PASSES - 1),
+            )
+
+        def mm_a(bank, a, t, u):
+            mm(bank, a, w1_w[:, a, t * P : (t + 1) * P], w1_s[:, a, t * P : (t + 1) * P], u, FP8X4)
+
+        def mm_b(bank, a, t, u):
+            mm(bank, a, w2_w[:, a, 2 * t * P : 2 * (t + 1) * P], w2_s[:, a, t * P : (t + 1) * P], u, FP4X4)
+
+        h = [held("h%d" % u, [P, PACK, HALF], F32) for u in range(HALVES)]
+        h_bf = [held("h_bf%d" % u, [P, HALF * PACK], BF16) for u in range(HALVES)]
+        h_w = [held("h_w%d" % u, [P, HALF], U32) for u in range(HALVES)]
+        h_s = held("h_s", [P, S], U8)
+        h_rows = out_1.rearrange("(p t) j -> p t j", t=PACK)
+        h_codes = out_2[0].rearrange("p m i -> p (m i)").bitcast(I32)
+
+        def combine(a_bank, b_bank, t, u):
+            sq = work.tile([P, HALF], F32, name="sq")
+            nc.scalar.activation(sq[:], a_bank[:], ACT.Square)
+            nc.vector.scalar_tensor_tensor(h[u][:, t, :], sq[:], gain_t[:, t : t + 1], b_bank[:], ALU.mult, ALU.add)
+
+        def round_h(u):
+            nc.sync.dma_start(h_rows[:, :, u * HALF : (u + 1) * HALF], h[u][:])
+            nc.vector.tensor_copy(
+                h_bf[u][:].rearrange("p (c i t) -> p c t i", i=4, t=PACK),
+                h[u][:].rearrange("p t (c i) -> p c t i", i=4),
+            )
+
+        def quantise_h(u):
+            nc.vector.quantize_mx(out=h_w[u][:].bitcast(FP8X4), scales=h_s[:, u * HALF : (u + 1) * HALF], in_=h_bf[u][:])
+            nc.sync.dma_start(h_codes[:, u * HALF : (u + 1) * HALF], h_w[u][:].bitcast(I32))
+
+        def second(n, u, square_on_scalar):
+            cols = slice(n * P, (n + 1) * P)
+            q_bank = psum.tile([P, HALF], F32, name="bank")
+            c_bank = psum.tile([P, HALF], F32, name="bank")
+            nc.tensor.matmul_mx(
+                out=q_bank[:], lhsT=w4_w[:, cols].bitcast(FP8X4), lhsT_scale=w4_s[:, cols],
+                rhs=h_w[u][:].bitcast(FP8X4), rhs_scale=h_s[:, u * HALF : (u + 1) * HALF], start=True, stop=True,
+            )
+            for a in range(PASSES):
+                mm(c_bank, a, w3_w[:, a, cols], w3_s[:, a * N + n * P : a * N + (n + 1) * P], u, FP8X4)
+            mag = work.tile([P, HALF], F32, name="mag")
+            root = work.tile([P, HALF], F32, name="root")
+            part = work.tile([P, HALF], F32, name="part")
+            y = work.tile([P, HALF], F32, name="y")
+            nc.scalar.activation(mag[:], q_bank[:], ACT.Abs)
+            nc.scalar.activation(root[:], mag[:], ACT.Abs_reciprocal_sqrt, bias=1.0)
+            if square_on_scalar:
+                nc.scalar.activation(part[:], root[:], ACT.Square)
+                nc.vector.tensor_tensor(y[:], c_bank[:], part[:], ALU.mult)
+            else:
+                nc.vector.tensor_tensor(part[:], c_bank[:], root[:], ALU.mult)
+                nc.vector.tensor_tensor(y[:], part[:], root[:], ALU.mult)
+            nc.sync.dma_start(out_0[cols, u * HALF : (u + 1) * HALF], y[:])
+
+        banks = [(psum.tile([P, HALF], F32, name="bank"), psum.tile([P, HALF], F32, name="bank")) for t in range(PACK)]
+        for t in range(PACK):
+            mm_a(banks[t][0], 0, t, 0)
+            mm_b(banks[t][1], 0, t, 0)
+        for t in range(PACK):
+            mm_a(banks[t][0], 1, t, 0)
+            mm_b(banks[t][1], 1, t, 0)
+            combine(banks[t][0], banks[t][1], t, 0)
+        round_h(0)
+        nc.vector.quantize_mx(out=w4_w[:, 0:256].bitcast(FP8X4), scales=w4_s[:, 0:256], in_=w4_bf[:, 0:1024])
+        nc.vector.quantize_mx(out=w4_w[:, 256:N].bitcast(FP8X4), scales=w4_s[:, 256:N], in_=w4_bf[:, 1024 : N * PACK])
+        quantise_h(0)
+        for t in range(PACK):
+            a_bank = psum.tile([P, HALF], F32, name="bank")
+            b_bank = psum.tile([P, HALF], F32, name="bank")
+            for a in range(PASSES):
+                mm_a(a_bank, a, t, 1)
+            for a in range(PASSES):
+                mm_b(b_bank, a, t, 1)
+            combine(a_bank, b_bank, t, 1)
+        round_h(1)
+        second(0, 0, True)
+        quantise_h(1)
+        second(1, 0, True)
+        second(2, 0, True)
+        for q in range(4):
+            nc.sync.dma_start(out_3[0, 4 * q : 4 * q + 4, :].bitcast(I32), h_s[32 * q : 32 * q + 4, :].bitcast(I32))
+        for n in range(NT):
+            second(n, 1, False)

@@ -22,6 +22,10 @@ PASSES = K // (P * PACK)
 HALF = 512
 HALVES = S // HALF
 NT = N // P
+PIECES = ((0, 512), (512, 256), (768, 256))
+BANKS = (((0, 1), (2, 3), (4, 5)), ((6,), (7,), (0,)), ((2,), (4,), (1,)))
+HOW = ("SSV", "VVV", "VVV")
+W4 = "S"
 
 
 def tile_list_speckle_energy_kernel(
@@ -32,7 +36,7 @@ def tile_list_speckle_energy_kernel(
     with ExitStack() as ctx:
         keep = ctx.enter_context(tc.tile_pool(name="keep", bufs=1))
         work = ctx.enter_context(tc.tile_pool(name="work", bufs=3))
-        psum = ctx.enter_context(tc.psum_pool(name="psum", bufs=8))
+        psum = ctx.enter_context(tc.psum_pool(name="psum", bufs=1))
 
         def held(name, shape, dtype):
             return keep.tile(shape, dtype, name=name, align_bytes=64)
@@ -41,64 +45,80 @@ def tile_list_speckle_energy_kernel(
         tab_s = held("tab_s", [P, T], U8)
         w2_s_raw = held("w2_s_raw", [P, PASSES * H], U8)
         w3_s = held("w3_s", [P, PASSES * N], U8)
-        v_s1 = held("v_s1", [P, S], U8)
+        v_planes = [held("v_s%d" % a, [P, S], U8) for a in range(PASSES)]
         one = held("one", [P, 1], F32)
         warm = held("warm", [P, 1], F32)
         nc.vector.memset(tab_s[:].bitcast(I32), 0)
         nc.vector.memset(one[:], 1.0)
         nc.vector.memset(w2_s_raw[:].bitcast(I32), 0)
         nc.vector.memset(w3_s[:].bitcast(I32), 0)
-        nc.vector.memset(v_s1[:].bitcast(I32), 0)
+        for plane in v_planes:
+            nc.vector.memset(plane[:].bitcast(I32), 0)
         nc.scalar.activation(warm[:], one[:], ACT.Abs_reciprocal_sqrt)
 
-        w1_raw = [held("w1_raw%d" % a, [P, PACK, H], F32) for a in range(PASSES)]
-        tab_w = [held("tab_w%d" % a, [P, T], U32) for a in range(PASSES)]
+        w1_raw0 = held("w1_raw0", [P, PACK, H], F32)
+        w1_raw1 = [held("w1_raw1%d" % g, [P, PACK, H // 2], F32) for g in range(2)]
+        tab_w = [held("tab_w0", [P, T], U32)]
+        tab_rows = tab_words.rearrange("a p t i -> a p (t i)").bitcast(I32)
         w2_w_raw = held("w2_w_raw", [P, PASSES, 2 * H], U8)
         gain_t = held("gain_t", [P, PACK], F32)
         w1_rows = w1.rearrange("(a p j) c -> a p j c", p=P, j=PACK)
-        nc.sync.dma_start(w1_raw[0][:], w1_rows[0])
-        nc.sync.dma_start(offsets[:], offs)
-        nc.sync.dma_start(gain_t[:], gain.rearrange("(p t) -> p t", t=PACK))
-        nc.sync.dma_start(w1_raw[1][:], w1_rows[1])
-        nc.sync.dma_start(w2_w_raw[:].bitcast(I32), w2_words.rearrange("a p c -> p a c").bitcast(I32))
-        for a in range(PASSES):
-            nc.sync.dma_start(tab_w[a][:].bitcast(I32), tab_words[a].rearrange("p t i -> p (t i)").bitcast(I32))
-        for q in range(4):
-            nc.gpsimd.dma_start(tab_s[32 * q : 32 * q + 8, :].bitcast(I32), tab_scales[:, 4 * q : 4 * q + 4, :].bitcast(I32))
-        for plane, scales in ((w2_s_raw, w2_scales), (w3_s, w3_scales)):
+
+        def load_plane(plane, scales):
             for q in range(4):
-                nc.gpsimd.dma_start(
+                nc.sync.dma_start(
                     plane[32 * q : 32 * q + 4, :].bitcast(I32).rearrange("r (a c) -> r a c", a=PASSES),
                     scales[:, 4 * q : 4 * q + 4, :].rearrange("a r c -> r a c").bitcast(I32),
                 )
 
+        nc.sync.dma_start(w1_raw0[:], w1_rows[0])
+        nc.sync.dma_start(tab_s[0:P:4, :].bitcast(I32), tab_scales.rearrange("a q t -> (a q) t").bitcast(I32))
+        nc.sync.dma_start(offsets[:], offs)
+        load_plane(w2_s_raw, w2_scales)
+        nc.sync.dma_start(tab_w[0][:].bitcast(I32), tab_rows[0])
+        nc.sync.dma_start(w2_w_raw[:].bitcast(I32), w2_words.rearrange("a p c -> p a c").bitcast(I32))
+
         w1_w = held("w1_w", [P, PASSES, H], U32)
         w1_s = held("w1_s", [P, PASSES, H], U8)
-        w1_bf = [held("w1_bf%d" % a, [P, H * PACK], BF16) for a in range(PASSES)]
-        for a in range(PASSES):
-            nc.scalar.copy(
-                w1_bf[a][:].rearrange("p (t m j) -> p m t j", t=PACK, j=PACK),
-                w1_raw[a][:].rearrange("p j (m t) -> p m t j", t=PACK),
-            )
+        w1_bf0 = held("w1_bf0", [P, H * PACK], BF16)
+        w1_bf1 = [held("w1_bf1%d" % e, [P, 2 * P * PACK], BF16) for e in range(2)]
+        nc.scalar.copy(
+            w1_bf0[:].rearrange("p (t m j) -> p m t j", t=PACK, j=PACK),
+            w1_raw0[:].rearrange("p j (m t) -> p m t j", t=PACK),
+        )
 
-        v_s = held("v_s", [P, S], U8)
-        nc.vector.tensor_copy(v_s[:], tab_s[:].indirect(offsets[:]))
-        for q in range(4):
-            nc.sync.dma_start(v_s1[32 * q : 32 * q + 4, :].bitcast(I32), v_s[32 * q + 4 : 32 * q + 8, :].bitcast(I32))
+        picked_s = held("picked_s", [P, S], U8)
+        nc.vector.tensor_copy(picked_s[:], tab_s[:].indirect(offsets[:]))
+
+        def move_plane(a):
+            for q in range(4):
+                first = 4 * (16 * a + 4 * q)
+                nc.sync.dma_start(v_planes[a][32 * q : 32 * q + 4, :].bitcast(I32), picked_s[first : first + 13 : 4, :].bitcast(I32))
+
+        move_plane(0)
+        tab_w.append(held("tab_s", [P, T], U32))
+        nc.sync.dma_start(tab_w[1][:].bitcast(I32), tab_rows[1])
+        move_plane(1)
+        for g in range(2):
+            nc.sync.dma_start(w1_raw1[g][:], w1_rows[1][:, :, g * H // 2 : (g + 1) * H // 2])
+        nc.sync.dma_start(gain_t[:], gain.rearrange("(p t) -> p t", t=PACK))
         w4_raw = held("w1_raw0", [P, PACK, N], F32)
-        w3_w = held("w1_raw1", [P, PASSES, N], U32)
+        w3_w = held("w3_w", [P, PASSES, N], U32)
         nc.sync.dma_start(w4_raw[:], w4.rearrange("(p j) n -> p j n", j=PACK))
         nc.sync.dma_start(w3_w[:].bitcast(I32), w3_words.rearrange("a p n i -> p a (n i)").bitcast(I32))
-        v_planes = [v_s, v_s1]
+        load_plane(w3_s, w3_scales)
 
         w2_w = held("w2_w", [P, PASSES, 2 * H], U8)
         w2_s = held("w2_s", [P, PASSES, H], U8)
         nc.vector.tensor_copy(
+            w2_s[:].rearrange("p a (t m) -> p a t m", t=PACK),
+            w2_s_raw[:].rearrange("p (a m t) -> p a t m", a=PASSES, t=PACK),
+        )
+        nc.vector.tensor_copy(
             w2_w[:].rearrange("p a (t m b) -> p a t m b", t=PACK, b=2),
             w2_w_raw[:].rearrange("p a (m t b) -> p a t m b", t=PACK, b=2),
         )
-        nc.vector.quantize_mx(out=w1_w[:, 0, :].bitcast(FP8X4), scales=w1_s[:, 0, :], in_=w1_bf[0][:])
-        nc.vector.quantize_mx(out=w1_w[:, 1, :].bitcast(FP8X4), scales=w1_s[:, 1, :], in_=w1_bf[1][:])
+        nc.vector.quantize_mx(out=w1_w[:, 0, :].bitcast(FP8X4), scales=w1_s[:, 0, :], in_=w1_bf0[:])
 
         v_w = [[held("v_w%d%d" % (a, u), [P, HALF], U32) for u in range(HALVES)] for a in range(PASSES)]
 
@@ -107,22 +127,43 @@ def tile_list_speckle_energy_kernel(
             nc.vector.tensor_copy(v_w[a][u][:], tab_w[a][:].indirect(offsets[:, u * cols : (u + 1) * cols]))
 
         gather(0, 0)
-        nc.vector.tensor_copy(
-            w2_s[:].rearrange("p a (t m) -> p a t m", t=PACK),
-            w2_s_raw[:].rearrange("p (a m t) -> p a t m", a=PASSES, t=PACK),
-        )
         gather(0, 1)
         gather(1, 0)
         gather(1, 1)
 
+        def round_w1(copy, e, g):
+            copy(
+                w1_bf1[e][:].rearrange("p (t m j) -> p m t j", t=2, j=PACK)[:, g * P // 2 : (g + 1) * P // 2],
+                w1_raw1[g][:].rearrange("p j (m t) -> p m t j", t=PACK)[:, :, 2 * e : 2 * e + 2],
+            )
+
+        round_w1(nc.scalar.copy, 0, 0)
+        round_w1(nc.scalar.copy, 1, 0)
+        round_w1(nc.vector.tensor_copy, 0, 1)
+        round_w1(nc.scalar.copy, 1, 1)
+        for e in range(2):
+            cols = slice(2 * e * P, 2 * (e + 1) * P)
+            nc.vector.quantize_mx(out=w1_w[:, 1, cols].bitcast(FP8X4), scales=w1_s[:, 1, cols], in_=w1_bf1[e][:])
+
         w4_bf = held("w4_bf", [P, N * PACK], BF16)
         w4_w = held("w4_w", [P, N], U32)
         w4_s = held("w4_s", [P, N], U8)
-        nc.gpsimd.tensor_scalar(
-            w4_bf[:].rearrange("p (c i j) -> p c j i", i=4, j=PACK),
-            w4_raw[:].rearrange("p j (c i) -> p c j i", i=4),
-            1.0, 0.0, ALU.mult, ALU.add,
-        )
+
+
+        def quantise_w4(n):
+            cols = slice(n * P, (n + 1) * P)
+            wide = slice(n * P * PACK, (n + 1) * P * PACK)
+            if W4 == "G":
+                nc.gpsimd.tensor_scalar(
+                    w4_bf[:, wide].rearrange("p (c j) -> p c j", j=PACK), w4_raw[:, :, cols].rearrange("p j c -> p c j"),
+                    1.0, 0.0, ALU.mult, ALU.add,
+                )
+            else:
+                nc.scalar.copy(
+                    w4_bf[:, wide].rearrange("p (c i j) -> p c j i", i=4, j=PACK),
+                    w4_raw[:, :, cols].rearrange("p j (c i) -> p c j i", i=4),
+                )
+            nc.vector.quantize_mx(out=w4_w[:, cols].bitcast(FP8X4), scales=w4_s[:, cols], in_=w4_bf[:, wide])
 
         def mm(bank, a, words, scales, u, dtype):
             nc.tensor.matmul_mx(
@@ -138,78 +179,137 @@ def tile_list_speckle_energy_kernel(
             mm(bank, a, w2_w[:, a, 2 * t * P : 2 * (t + 1) * P], w2_s[:, a, t * P : (t + 1) * P], u, FP4X4)
 
         h = [held("h%d" % u, [P, PACK, HALF], F32) for u in range(HALVES)]
-        h_bf = [held("h_bf%d" % u, [P, HALF * PACK], BF16) for u in range(HALVES)]
-        h_w = [held("h_w%d" % u, [P, HALF], U32) for u in range(HALVES)]
+        h_bf = [held("h_bf%d" % k, [P, width * PACK], BF16) for k, (first, width) in enumerate(PIECES)]
+        h_w = [held("h_w%d" % k, [P, width], U32) for k, (first, width) in enumerate(PIECES)]
         h_s = held("h_s", [P, S], U8)
         h_rows = out_1.rearrange("(p t) j -> p t j", t=PACK)
         h_codes = out_2[0].rearrange("p m i -> p (m i)").bitcast(I32)
 
-        def combine(a_bank, b_bank, t, u):
-            sq = work.tile([P, HALF], F32, name="sq")
+        def bank(i):
+            return psum.tile([P, HALF], F32, name="bank%d" % i)
+
+        def square(a_bank):
+            sq = work.tile([P, HALF], F32, name="sq", bufs=5)
             nc.scalar.activation(sq[:], a_bank[:], ACT.Square)
+            return sq
+
+        def combine(sq, b_bank, t, u):
             nc.vector.scalar_tensor_tensor(h[u][:, t, :], sq[:], gain_t[:, t : t + 1], b_bank[:], ALU.mult, ALU.add)
 
-        def round_h(u):
+        def store_h(u):
             nc.sync.dma_start(h_rows[:, :, u * HALF : (u + 1) * HALF], h[u][:])
+
+        def round_h(k):
+            first, width = PIECES[k]
+            u, inner = divmod(first, HALF)
             nc.vector.tensor_copy(
-                h_bf[u][:].rearrange("p (c i t) -> p c t i", i=4, t=PACK),
-                h[u][:].rearrange("p t (c i) -> p c t i", i=4),
+                h_bf[k][:].rearrange("p (c i t) -> p c t i", i=4, t=PACK),
+                h[u][:, :, inner : inner + width].rearrange("p t (c i) -> p c t i", i=4),
             )
 
-        def quantise_h(u):
-            nc.vector.quantize_mx(out=h_w[u][:].bitcast(FP8X4), scales=h_s[:, u * HALF : (u + 1) * HALF], in_=h_bf[u][:])
-            nc.sync.dma_start(h_codes[:, u * HALF : (u + 1) * HALF], h_w[u][:].bitcast(I32))
+        def quantise_h(k):
+            first, width = PIECES[k]
+            cols = slice(first, first + width)
+            nc.vector.quantize_mx(out=h_w[k][:].bitcast(FP8X4), scales=h_s[:, cols], in_=h_bf[k][:])
+            nc.sync.dma_start(h_codes[:, cols], h_w[k][:].bitcast(I32))
 
-        def second(n, u, square_on_scalar):
-            cols = slice(n * P, (n + 1) * P)
-            q_bank = psum.tile([P, HALF], F32, name="bank")
-            c_bank = psum.tile([P, HALF], F32, name="bank")
-            nc.tensor.matmul_mx(
-                out=q_bank[:], lhsT=w4_w[:, cols].bitcast(FP8X4), lhsT_scale=w4_s[:, cols],
-                rhs=h_w[u][:].bitcast(FP8X4), rhs_scale=h_s[:, u * HALF : (u + 1) * HALF], start=True, stop=True,
-            )
+        def front(n, k):
+            first, width = PIECES[k]
+            rows = slice(n * P, (n + 1) * P)
+            cols = slice(first, first + width)
+            u, inner = divmod(first, HALF)
+            banks = [bank(i) for i in BANKS[k][n]]
+            q_sum = banks[0][:, :width]
+            c_sum = banks[-1][:, HALF - width :]
             for a in range(PASSES):
-                mm(c_bank, a, w3_w[:, a, cols], w3_s[:, a * N + n * P : a * N + (n + 1) * P], u, FP8X4)
-            mag = work.tile([P, HALF], F32, name="mag")
-            root = work.tile([P, HALF], F32, name="root")
-            part = work.tile([P, HALF], F32, name="part")
-            y = work.tile([P, HALF], F32, name="y")
-            nc.scalar.activation(mag[:], q_bank[:], ACT.Abs)
+                nc.tensor.matmul_mx(
+                    out=c_sum, lhsT=w3_w[:, a, rows].bitcast(FP8X4),
+                    lhsT_scale=w3_s[:, a * N + n * P : a * N + (n + 1) * P],
+                    rhs=v_w[a][u][:, inner : inner + width].bitcast(FP8X4), rhs_scale=v_planes[a][:, cols],
+                    start=(a == 0), stop=(a == PASSES - 1),
+                )
+            nc.tensor.matmul_mx(
+                out=q_sum, lhsT=w4_w[:, rows].bitcast(FP8X4), lhsT_scale=w4_s[:, rows],
+                rhs=h_w[k][:].bitcast(FP8X4), rhs_scale=h_s[:, cols], start=True, stop=True,
+            )
+            mag = work.tile([P, width], F32, name="mag")
+            root = work.tile([P, width], F32, name="root", bufs=9)
+            nc.scalar.activation(mag[:], q_sum, ACT.Abs)
             nc.scalar.activation(root[:], mag[:], ACT.Abs_reciprocal_sqrt, bias=1.0)
-            if square_on_scalar:
-                nc.scalar.activation(part[:], root[:], ACT.Square)
-                nc.vector.tensor_tensor(y[:], c_bank[:], part[:], ALU.mult)
-            else:
-                nc.vector.tensor_tensor(part[:], c_bank[:], root[:], ALU.mult)
-                nc.vector.tensor_tensor(y[:], part[:], root[:], ALU.mult)
-            nc.sync.dma_start(out_0[cols, u * HALF : (u + 1) * HALF], y[:])
+            return c_sum, root
 
-        banks = [(psum.tile([P, HALF], F32, name="bank"), psum.tile([P, HALF], F32, name="bank")) for t in range(PACK)]
+        def back(n, k, c_sum, root):
+            first, width = PIECES[k]
+            how = HOW[k][n]
+            part = work.tile([P, width], F32, name="part", bufs=6)
+            y = work.tile([P, width], F32, name="y", bufs=9)
+            if how == "S":
+                nc.scalar.activation(part[:], root[:], ACT.Square)
+                nc.vector.tensor_tensor(y[:], c_sum, part[:], ALU.mult)
+            elif how == "G":
+                nc.gpsimd.tensor_tensor(part[:], root[:], root[:], ALU.mult)
+                nc.vector.tensor_tensor(y[:], c_sum, part[:], ALU.mult)
+            else:
+                nc.vector.tensor_tensor(part[:], c_sum, root[:], ALU.mult)
+                nc.vector.tensor_tensor(y[:], part[:], root[:], ALU.mult)
+            nc.sync.dma_start(out_0[n * P : (n + 1) * P, first : first + width], y[:])
+
+        a_banks = [bank(t) for t in range(PACK)]
+        b_banks = [bank(PACK + t) for t in range(PACK)]
         for t in range(PACK):
-            mm_a(banks[t][0], 0, t, 0)
-            mm_b(banks[t][1], 0, t, 0)
+            mm_a(a_banks[t], 0, t, 0)
+        for a in range(PASSES):
+            for t in range(PACK):
+                mm_b(b_banks[t], a, t, 0)
         for t in range(PACK):
-            mm_a(banks[t][0], 1, t, 0)
-            mm_b(banks[t][1], 1, t, 0)
-            combine(banks[t][0], banks[t][1], t, 0)
-        round_h(0)
-        nc.vector.quantize_mx(out=w4_w[:, 0:256].bitcast(FP8X4), scales=w4_s[:, 0:256], in_=w4_bf[:, 0:1024])
-        nc.vector.quantize_mx(out=w4_w[:, 256:N].bitcast(FP8X4), scales=w4_s[:, 256:N], in_=w4_bf[:, 1024 : N * PACK])
-        quantise_h(0)
-        for t in range(PACK):
-            a_bank = psum.tile([P, HALF], F32, name="bank")
-            b_bank = psum.tile([P, HALF], F32, name="bank")
+            mm_a(a_banks[t], 1, t, 0)
+            combine(square(a_banks[t]), b_banks[t], t, 0)
+        squares = []
+        b_banks = []
+
+        def first_a(t):
+            a_bank = bank(t)
             for a in range(PASSES):
                 mm_a(a_bank, a, t, 1)
+            squares.append(square(a_bank))
+
+        def first_b(t):
+            b_banks.append(bank(PACK + t))
             for a in range(PASSES):
-                mm_b(b_bank, a, t, 1)
-            combine(a_bank, b_bank, t, 1)
+                mm_b(b_banks[t], a, t, 1)
+
+        store_h(0)
+        round_h(0)
+        quantise_w4(0)
+        quantise_h(0)
+        first_a(0)
+        first_a(1)
+        first_b(0)
+        first_a(2)
+        first_a(3)
+        first_b(1)
+        quantise_w4(1)
+        parts0 = [front(0, 0), front(1, 0)]
+        first_b(2)
+        first_b(3)
+        for t in range(PACK):
+            combine(squares[t], b_banks[t], t, 1)
+        quantise_w4(2)
+        parts0.append(front(2, 0))
+        store_h(1)
         round_h(1)
-        second(0, 0, True)
+        round_h(2)
         quantise_h(1)
-        second(1, 0, True)
-        second(2, 0, True)
+        quantise_h(2)
+        parts1 = [front(n, 1) for n in range(NT)]
+        parts2 = [front(n, 2) for n in range(2)]
+        back(0, 0, parts0[0][0], parts0[0][1])
+        parts2.append(front(2, 2))
         for q in range(4):
             nc.sync.dma_start(out_3[0, 4 * q : 4 * q + 4, :].bitcast(I32), h_s[32 * q : 32 * q + 4, :].bitcast(I32))
+        for n in (1, 2):
+            back(n, 0, parts0[n][0], parts0[n][1])
         for n in range(NT):
-            second(n, 1, False)
+            back(n, 1, parts1[n][0], parts1[n][1])
+        for n in range(NT):
+            back(n, 2, parts2[n][0], parts2[n][1])

@@ -18,14 +18,15 @@ ALU = mybir.AluOpType
 
 P = 128
 PACK = 4
+QUADS = 4
 PASSES = K // (P * PACK)
 HALF = 512
 HALVES = S // HALF
-NT = N // P
-PIECES = ((0, 512), (512, 256), (768, 256))
+ROW_TILES = N // P
+
+PIECES = ((0, HALF), (HALF, HALF // 2), (HALF + HALF // 2, HALF // 2))
 BANKS = (((0, 1), (2, 3), (4, 5)), ((6,), (7,), (0,)), ((2,), (4,), (1,)))
-HOW = ("SSV", "VVV", "VVV")
-W4 = "S"
+SCALAR_SQUARES = 2
 
 
 def tile_list_speckle_energy_kernel(
@@ -33,80 +34,84 @@ def tile_list_speckle_energy_kernel(
     out_0, out_1, out_2, out_3,
 ):
     nc = tc.nc
+    y_tiles = len(PIECES) * ROW_TILES
     with ExitStack() as ctx:
         keep = ctx.enter_context(tc.tile_pool(name="keep", bufs=1))
-        work = ctx.enter_context(tc.tile_pool(name="work", bufs=3))
+        work = ctx.enter_context(tc.tile_pool(name="work", bufs=1))
         psum = ctx.enter_context(tc.psum_pool(name="psum", bufs=1))
 
         def held(name, shape, dtype):
             return keep.tile(shape, dtype, name=name, align_bytes=64)
 
+        def bank(index):
+            return psum.tile([P, HALF], F32, name="bank%d" % index)
+
         offsets = keep.tile([P, S // 16], U16, name="offsets")
-        tab_s = held("tab_s", [P, T], U8)
+        tab_s = held("table_buffer", [P, T], U8)
         w2_s_raw = held("w2_s_raw", [P, PASSES * H], U8)
         w3_s = held("w3_s", [P, PASSES * N], U8)
-        v_planes = [held("v_s%d" % a, [P, S], U8) for a in range(PASSES)]
-        one = held("one", [P, 1], F32)
-        warm = held("warm", [P, 1], F32)
+        v_planes = [held("v_plane%d" % a, [P, S], U8) for a in range(PASSES)]
         nc.vector.memset(tab_s[:].bitcast(I32), 0)
+        one = held("one", [P, 1], F32)
         nc.vector.memset(one[:], 1.0)
         nc.vector.memset(w2_s_raw[:].bitcast(I32), 0)
         nc.vector.memset(w3_s[:].bitcast(I32), 0)
         for plane in v_planes:
             nc.vector.memset(plane[:].bitcast(I32), 0)
+        warm = held("warm", [P, 1], F32)
         nc.scalar.activation(warm[:], one[:], ACT.Abs_reciprocal_sqrt)
 
-        w1_raw0 = held("w1_raw0", [P, PACK, H], F32)
-        w1_raw1 = [held("w1_raw1%d" % g, [P, PACK, H // 2], F32) for g in range(2)]
-        tab_w = [held("tab_w0", [P, T], U32)]
-        tab_rows = tab_words.rearrange("a p t i -> a p (t i)").bitcast(I32)
-        w2_w_raw = held("w2_w_raw", [P, PASSES, 2 * H], U8)
-        gain_t = held("gain_t", [P, PACK], F32)
-        w1_rows = w1.rearrange("(a p j) c -> a p j c", p=P, j=PACK)
-
-        def load_plane(plane, scales):
-            for q in range(4):
+        def load_planes(planes, scales):
+            for quad in range(QUADS):
                 nc.sync.dma_start(
-                    plane[32 * q : 32 * q + 4, :].bitcast(I32).rearrange("r (a c) -> r a c", a=PASSES),
-                    scales[:, 4 * q : 4 * q + 4, :].rearrange("a r c -> r a c").bitcast(I32),
+                    planes[32 * quad : 32 * quad + 4, :].bitcast(I32).rearrange("s (a c) -> s a c", a=PASSES),
+                    scales[:, 4 * quad : 4 * quad + 4, :].rearrange("a s c -> s a c").bitcast(I32),
                 )
 
+        w1_rows = w1.rearrange("(a p i) c -> a p i c", p=P, i=PACK)
+        tab_rows = tab_words.rearrange("a p t i -> a p (t i)").bitcast(I32)
+        w1_raw0 = held("weight_buffer", [P, PACK, H], F32)
+        w1_raw1 = held("w1_raw1", [P, PACK, H], F32)
+        tab_w0 = held("tab_w0", [P, T], U32)
+        w2_w_raw = held("w2_w_raw", [P, PASSES, 2 * H], U8)
+        gain_t = held("gain_t", [P, PACK], F32)
         nc.sync.dma_start(w1_raw0[:], w1_rows[0])
         nc.sync.dma_start(tab_s[0:P:4, :].bitcast(I32), tab_scales.rearrange("a q t -> (a q) t").bitcast(I32))
         nc.sync.dma_start(offsets[:], offs)
-        load_plane(w2_s_raw, w2_scales)
-        nc.sync.dma_start(tab_w[0][:].bitcast(I32), tab_rows[0])
+        load_planes(w2_s_raw, w2_scales)
+        nc.sync.dma_start(tab_w0[:].bitcast(I32), tab_rows[0])
         nc.sync.dma_start(w2_w_raw[:].bitcast(I32), w2_words.rearrange("a p c -> p a c").bitcast(I32))
 
         w1_w = held("w1_w", [P, PASSES, H], U32)
         w1_s = held("w1_s", [P, PASSES, H], U8)
         w1_bf0 = held("w1_bf0", [P, H * PACK], BF16)
-        w1_bf1 = [held("w1_bf1%d" % e, [P, 2 * P * PACK], BF16) for e in range(2)]
         nc.scalar.copy(
-            w1_bf0[:].rearrange("p (t m j) -> p m t j", t=PACK, j=PACK),
-            w1_raw0[:].rearrange("p j (m t) -> p m t j", t=PACK),
+            w1_bf0[:].rearrange("p (t m i) -> p m t i", t=PACK, i=PACK),
+            w1_raw0[:].rearrange("p i (m t) -> p m t i", t=PACK),
         )
 
         picked_s = held("picked_s", [P, S], U8)
         nc.vector.tensor_copy(picked_s[:], tab_s[:].indirect(offsets[:]))
 
         def move_plane(a):
-            for q in range(4):
-                first = 4 * (16 * a + 4 * q)
-                nc.sync.dma_start(v_planes[a][32 * q : 32 * q + 4, :].bitcast(I32), picked_s[first : first + 13 : 4, :].bitcast(I32))
+            for quad in range(QUADS):
+                first = 4 * (16 * a + 4 * quad)
+                nc.sync.dma_start(
+                    v_planes[a][32 * quad : 32 * quad + 4, :].bitcast(I32),
+                    picked_s[first : first + 13 : 4, :].bitcast(I32),
+                )
 
         move_plane(0)
-        tab_w.append(held("tab_s", [P, T], U32))
-        nc.sync.dma_start(tab_w[1][:].bitcast(I32), tab_rows[1])
+        tab_w1 = held("table_buffer", [P, T], U32)
+        nc.sync.dma_start(tab_w1[:].bitcast(I32), tab_rows[1])
         move_plane(1)
-        for g in range(2):
-            nc.sync.dma_start(w1_raw1[g][:], w1_rows[1][:, :, g * H // 2 : (g + 1) * H // 2])
+        nc.sync.dma_start(w1_raw1[:], w1_rows[1])
         nc.sync.dma_start(gain_t[:], gain.rearrange("(p t) -> p t", t=PACK))
-        w4_raw = held("w1_raw0", [P, PACK, N], F32)
+        w4_raw = held("weight_buffer", [P, PACK, N], F32)
         w3_w = held("w3_w", [P, PASSES, N], U32)
-        nc.sync.dma_start(w4_raw[:], w4.rearrange("(p j) n -> p j n", j=PACK))
+        nc.sync.dma_start(w4_raw[:], w4.rearrange("(p i) n -> p i n", i=PACK))
         nc.sync.dma_start(w3_w[:].bitcast(I32), w3_words.rearrange("a p n i -> p a (n i)").bitcast(I32))
-        load_plane(w3_s, w3_scales)
+        load_planes(w3_s, w3_scales)
 
         w2_w = held("w2_w", [P, PASSES, 2 * H], U8)
         w2_s = held("w2_s", [P, PASSES, H], U8)
@@ -121,62 +126,50 @@ def tile_list_speckle_energy_kernel(
         nc.vector.quantize_mx(out=w1_w[:, 0, :].bitcast(FP8X4), scales=w1_s[:, 0, :], in_=w1_bf0[:])
 
         v_w = [[held("v_w%d%d" % (a, u), [P, HALF], U32) for u in range(HALVES)] for a in range(PASSES)]
+        for a, tab_w in enumerate((tab_w0, tab_w1)):
+            for u in range(HALVES):
+                entries = offsets[:, u * HALF // 16 : (u + 1) * HALF // 16]
+                nc.vector.tensor_copy(v_w[a][u][:], tab_w[:].indirect(entries))
 
-        def gather(a, u):
-            cols = HALF // 16
-            nc.vector.tensor_copy(v_w[a][u][:], tab_w[a][:].indirect(offsets[:, u * cols : (u + 1) * cols]))
-
-        gather(0, 0)
-        gather(0, 1)
-        gather(1, 0)
-        gather(1, 1)
-
-        def round_w1(copy, e, g):
+        w1_bf1 = [held("w1_bf1%d" % pair, [P, 2 * P * PACK], BF16) for pair in range(2)]
+        for pair, copy in enumerate((nc.vector.tensor_copy, nc.scalar.copy)):
             copy(
-                w1_bf1[e][:].rearrange("p (t m j) -> p m t j", t=2, j=PACK)[:, g * P // 2 : (g + 1) * P // 2],
-                w1_raw1[g][:].rearrange("p j (m t) -> p m t j", t=PACK)[:, :, 2 * e : 2 * e + 2],
+                w1_bf1[pair][:].rearrange("p (t m i) -> p m t i", t=2, i=PACK),
+                w1_raw1[:].rearrange("p i (m t) -> p m t i", t=PACK)[:, :, 2 * pair : 2 * pair + 2],
             )
-
-        round_w1(nc.scalar.copy, 0, 0)
-        round_w1(nc.scalar.copy, 1, 0)
-        round_w1(nc.vector.tensor_copy, 0, 1)
-        round_w1(nc.scalar.copy, 1, 1)
-        for e in range(2):
-            cols = slice(2 * e * P, 2 * (e + 1) * P)
-            nc.vector.quantize_mx(out=w1_w[:, 1, cols].bitcast(FP8X4), scales=w1_s[:, 1, cols], in_=w1_bf1[e][:])
+        for pair in range(2):
+            cols = slice(2 * pair * P, 2 * (pair + 1) * P)
+            nc.vector.quantize_mx(out=w1_w[:, 1, cols].bitcast(FP8X4), scales=w1_s[:, 1, cols], in_=w1_bf1[pair][:])
 
         w4_bf = held("w4_bf", [P, N * PACK], BF16)
         w4_w = held("w4_w", [P, N], U32)
         w4_s = held("w4_s", [P, N], U8)
 
-
         def quantise_w4(n):
             cols = slice(n * P, (n + 1) * P)
             wide = slice(n * P * PACK, (n + 1) * P * PACK)
-            if W4 == "G":
-                nc.gpsimd.tensor_scalar(
-                    w4_bf[:, wide].rearrange("p (c j) -> p c j", j=PACK), w4_raw[:, :, cols].rearrange("p j c -> p c j"),
-                    1.0, 0.0, ALU.mult, ALU.add,
-                )
-            else:
-                nc.scalar.copy(
-                    w4_bf[:, wide].rearrange("p (c i j) -> p c j i", i=4, j=PACK),
-                    w4_raw[:, :, cols].rearrange("p j (c i) -> p c j i", i=4),
-                )
+            nc.scalar.copy(
+                w4_bf[:, wide].rearrange("p (c e i) -> p c i e", e=4, i=PACK),
+                w4_raw[:, :, cols].rearrange("p i (c e) -> p c i e", e=4),
+            )
             nc.vector.quantize_mx(out=w4_w[:, cols].bitcast(FP8X4), scales=w4_s[:, cols], in_=w4_bf[:, wide])
 
-        def mm(bank, a, words, scales, u, dtype):
+        def pass_over_v(out, a, words, scales, first, width):
+            u, inner = divmod(first, HALF)
             nc.tensor.matmul_mx(
-                out=bank[:], lhsT=words.bitcast(dtype), lhsT_scale=scales,
-                rhs=v_w[a][u][:].bitcast(FP8X4), rhs_scale=v_planes[a][:, u * HALF : (u + 1) * HALF],
+                out=out, lhsT=words, lhsT_scale=scales,
+                rhs=v_w[a][u][:, inner : inner + width].bitcast(FP8X4),
+                rhs_scale=v_planes[a][:, first : first + width],
                 start=(a == 0), stop=(a == PASSES - 1),
             )
 
-        def mm_a(bank, a, t, u):
-            mm(bank, a, w1_w[:, a, t * P : (t + 1) * P], w1_s[:, a, t * P : (t + 1) * P], u, FP8X4)
+        def w1_pass(w1_bank, a, t, u):
+            cols = slice(t * P, (t + 1) * P)
+            pass_over_v(w1_bank[:], a, w1_w[:, a, cols].bitcast(FP8X4), w1_s[:, a, cols], u * HALF, HALF)
 
-        def mm_b(bank, a, t, u):
-            mm(bank, a, w2_w[:, a, 2 * t * P : 2 * (t + 1) * P], w2_s[:, a, t * P : (t + 1) * P], u, FP4X4)
+        def w2_pass(w2_bank, a, t, u):
+            words = w2_w[:, a, 2 * t * P : 2 * (t + 1) * P].bitcast(FP4X4)
+            pass_over_v(w2_bank[:], a, words, w2_s[:, a, t * P : (t + 1) * P], u * HALF, HALF)
 
         h = [held("h%d" % u, [P, PACK, HALF], F32) for u in range(HALVES)]
         h_bf = [held("h_bf%d" % k, [P, width * PACK], BF16) for k, (first, width) in enumerate(PIECES)]
@@ -185,16 +178,15 @@ def tile_list_speckle_energy_kernel(
         h_rows = out_1.rearrange("(p t) j -> p t j", t=PACK)
         h_codes = out_2[0].rearrange("p m i -> p (m i)").bitcast(I32)
 
-        def bank(i):
-            return psum.tile([P, HALF], F32, name="bank%d" % i)
+        def square(w1_bank):
+            squared = work.tile([P, HALF], F32, name="squared", bufs=PACK + 1)
+            nc.scalar.activation(squared[:], w1_bank[:], ACT.Square)
+            return squared
 
-        def square(a_bank):
-            sq = work.tile([P, HALF], F32, name="sq", bufs=5)
-            nc.scalar.activation(sq[:], a_bank[:], ACT.Square)
-            return sq
-
-        def combine(sq, b_bank, t, u):
-            nc.vector.scalar_tensor_tensor(h[u][:, t, :], sq[:], gain_t[:, t : t + 1], b_bank[:], ALU.mult, ALU.add)
+        def combine(squared, w2_bank, t, u):
+            nc.vector.scalar_tensor_tensor(
+                h[u][:, t, :], squared[:], gain_t[:, t : t + 1], w2_bank[:], ALU.mult, ALU.add
+            )
 
         def store_h(u):
             nc.sync.dma_start(h_rows[:, :, u * HALF : (u + 1) * HALF], h[u][:])
@@ -203,8 +195,8 @@ def tile_list_speckle_energy_kernel(
             first, width = PIECES[k]
             u, inner = divmod(first, HALF)
             nc.vector.tensor_copy(
-                h_bf[k][:].rearrange("p (c i t) -> p c t i", i=4, t=PACK),
-                h[u][:, :, inner : inner + width].rearrange("p t (c i) -> p c t i", i=4),
+                h_bf[k][:].rearrange("p (c e t) -> p c t e", e=4, t=PACK),
+                h[u][:, :, inner : inner + width].rearrange("p t (c e) -> p c t e", e=4),
             )
 
         def quantise_h(k):
@@ -213,103 +205,98 @@ def tile_list_speckle_energy_kernel(
             nc.vector.quantize_mx(out=h_w[k][:].bitcast(FP8X4), scales=h_s[:, cols], in_=h_bf[k][:])
             nc.sync.dma_start(h_codes[:, cols], h_w[k][:].bitcast(I32))
 
-        def front(n, k):
+        def scalar_squares(k, n):
+            place = k * ROW_TILES + n
+            return place < SCALAR_SQUARES or place >= y_tiles - SCALAR_SQUARES
+
+        def products(k, n):
             first, width = PIECES[k]
             rows = slice(n * P, (n + 1) * P)
-            cols = slice(first, first + width)
-            u, inner = divmod(first, HALF)
-            banks = [bank(i) for i in BANKS[k][n]]
+            banks = [bank(index) for index in BANKS[k][n]]
             q_sum = banks[0][:, :width]
             c_sum = banks[-1][:, HALF - width :]
             for a in range(PASSES):
-                nc.tensor.matmul_mx(
-                    out=c_sum, lhsT=w3_w[:, a, rows].bitcast(FP8X4),
-                    lhsT_scale=w3_s[:, a * N + n * P : a * N + (n + 1) * P],
-                    rhs=v_w[a][u][:, inner : inner + width].bitcast(FP8X4), rhs_scale=v_planes[a][:, cols],
-                    start=(a == 0), stop=(a == PASSES - 1),
-                )
+                scales = w3_s[:, a * N + n * P : a * N + (n + 1) * P]
+                pass_over_v(c_sum, a, w3_w[:, a, rows].bitcast(FP8X4), scales, first, width)
             nc.tensor.matmul_mx(
                 out=q_sum, lhsT=w4_w[:, rows].bitcast(FP8X4), lhsT_scale=w4_s[:, rows],
-                rhs=h_w[k][:].bitcast(FP8X4), rhs_scale=h_s[:, cols], start=True, stop=True,
+                rhs=h_w[k][:].bitcast(FP8X4), rhs_scale=h_s[:, first : first + width], start=True, stop=True,
             )
-            mag = work.tile([P, width], F32, name="mag")
-            root = work.tile([P, width], F32, name="root", bufs=9)
-            nc.scalar.activation(mag[:], q_sum, ACT.Abs)
-            nc.scalar.activation(root[:], mag[:], ACT.Abs_reciprocal_sqrt, bias=1.0)
+            magnitude = work.tile([P, width], F32, name="magnitude", bufs=ROW_TILES)
+            root = work.tile([P, width], F32, name="root", bufs=y_tiles)
+            nc.scalar.activation(magnitude[:], q_sum, ACT.Abs)
+            nc.scalar.activation(root[:], magnitude[:], ACT.Abs_reciprocal_sqrt, bias=1.0)
+            if scalar_squares(k, n):
+                inverse = work.tile([P, width], F32, name="inverse", bufs=2 * SCALAR_SQUARES)
+                nc.scalar.activation(inverse[:], root[:], ACT.Square)
+                return c_sum, inverse
             return c_sum, root
 
-        def back(n, k, c_sum, root):
+        def finish(k, n, c_sum, factor):
             first, width = PIECES[k]
-            how = HOW[k][n]
-            part = work.tile([P, width], F32, name="part", bufs=6)
-            y = work.tile([P, width], F32, name="y", bufs=9)
-            if how == "S":
-                nc.scalar.activation(part[:], root[:], ACT.Square)
-                nc.vector.tensor_tensor(y[:], c_sum, part[:], ALU.mult)
-            elif how == "G":
-                nc.gpsimd.tensor_tensor(part[:], root[:], root[:], ALU.mult)
-                nc.vector.tensor_tensor(y[:], c_sum, part[:], ALU.mult)
+            y = work.tile([P, width], F32, name="y", bufs=y_tiles)
+            if scalar_squares(k, n):
+                nc.vector.tensor_tensor(y[:], c_sum, factor[:], ALU.mult)
             else:
-                nc.vector.tensor_tensor(part[:], c_sum, root[:], ALU.mult)
-                nc.vector.tensor_tensor(y[:], part[:], root[:], ALU.mult)
+                once = work.tile([P, width], F32, name="once", bufs=y_tiles - 2 * SCALAR_SQUARES)
+                nc.vector.tensor_tensor(once[:], c_sum, factor[:], ALU.mult)
+                nc.vector.tensor_tensor(y[:], once[:], factor[:], ALU.mult)
             nc.sync.dma_start(out_0[n * P : (n + 1) * P, first : first + width], y[:])
 
-        a_banks = [bank(t) for t in range(PACK)]
-        b_banks = [bank(PACK + t) for t in range(PACK)]
+        w1_banks = [bank(t) for t in range(PACK)]
+        w2_banks = [bank(PACK + t) for t in range(PACK)]
         for t in range(PACK):
-            mm_a(a_banks[t], 0, t, 0)
+            w1_pass(w1_banks[t], 0, t, 0)
         for a in range(PASSES):
             for t in range(PACK):
-                mm_b(b_banks[t], a, t, 0)
+                w2_pass(w2_banks[t], a, t, 0)
         for t in range(PACK):
-            mm_a(a_banks[t], 1, t, 0)
-            combine(square(a_banks[t]), b_banks[t], t, 0)
-        squares = []
-        b_banks = []
-
-        def first_a(t):
-            a_bank = bank(t)
-            for a in range(PASSES):
-                mm_a(a_bank, a, t, 1)
-            squares.append(square(a_bank))
-
-        def first_b(t):
-            b_banks.append(bank(PACK + t))
-            for a in range(PASSES):
-                mm_b(b_banks[t], a, t, 1)
-
+            w1_pass(w1_banks[t], 1, t, 0)
+            combine(square(w1_banks[t]), w2_banks[t], t, 0)
         store_h(0)
         round_h(0)
         quantise_w4(0)
         quantise_h(0)
-        first_a(0)
-        first_a(1)
-        first_b(0)
-        first_a(2)
-        first_a(3)
-        first_b(1)
+
+        def w1_squared(t):
+            w1_bank = bank(t)
+            for a in range(PASSES):
+                w1_pass(w1_bank, a, t, 1)
+            return square(w1_bank)
+
+        def w2_product(t):
+            w2_bank = bank(PACK + t)
+            for a in range(PASSES):
+                w2_pass(w2_bank, a, t, 1)
+            return w2_bank
+
+        squares = []
+        w2_sums = []
+        for pair in range(2):
+            squares.extend([w1_squared(2 * pair), w1_squared(2 * pair + 1)])
+            w2_sums.append(w2_product(pair))
         quantise_w4(1)
-        parts0 = [front(0, 0), front(1, 0)]
-        first_b(2)
-        first_b(3)
+        pending = {(0, n): products(0, n) for n in range(2)}
+        w2_sums.extend([w2_product(2), w2_product(3)])
         for t in range(PACK):
-            combine(squares[t], b_banks[t], t, 1)
+            combine(squares[t], w2_sums[t], t, 1)
         quantise_w4(2)
-        parts0.append(front(2, 0))
+        pending[0, 2] = products(0, 2)
         store_h(1)
         round_h(1)
         round_h(2)
         quantise_h(1)
         quantise_h(2)
-        parts1 = [front(n, 1) for n in range(NT)]
-        parts2 = [front(n, 2) for n in range(2)]
-        back(0, 0, parts0[0][0], parts0[0][1])
-        parts2.append(front(2, 2))
-        for q in range(4):
-            nc.sync.dma_start(out_3[0, 4 * q : 4 * q + 4, :].bitcast(I32), h_s[32 * q : 32 * q + 4, :].bitcast(I32))
-        for n in (1, 2):
-            back(n, 0, parts0[n][0], parts0[n][1])
-        for n in range(NT):
-            back(n, 1, parts1[n][0], parts1[n][1])
-        for n in range(NT):
-            back(n, 2, parts2[n][0], parts2[n][1])
+
+        for n in range(ROW_TILES):
+            pending[1, n] = products(1, n)
+        for n in range(ROW_TILES - 1):
+            pending[2, n] = products(2, n)
+        finish(0, 0, *pending[0, 0])
+        pending[2, ROW_TILES - 1] = products(2, ROW_TILES - 1)
+        for quad in range(QUADS):
+            nc.sync.dma_start(
+                out_3[0, 4 * quad : 4 * quad + 4, :].bitcast(I32), h_s[32 * quad : 32 * quad + 4, :].bitcast(I32)
+            )
+        for k, n in sorted(pending)[1:]:
+            finish(k, n, *pending[k, n])

@@ -18,15 +18,15 @@ ALU = mybir.AluOpType
 
 P = 128
 PACK = 4
-QUADS = 4
 PASSES = K // (P * PACK)
 HALF = 512
 HALVES = S // HALF
 ROW_TILES = N // P
 
-PIECES = ((0, HALF), (HALF, HALF // 2), (HALF + HALF // 2, HALF // 2))
-BANKS = (((0, 1), (2, 3), (4, 5)), ((6,), (7,), (0,)), ((2,), (4,), (1,)))
-SCALAR_SQUARES = 2
+PIECE = HALF // 2
+PIECES = S // PIECE
+BY_GPSIMD = ((1, 0), (1, 1), (2, 0), (2, 1))
+C_BANKS = ((3, 4, 5), (6, 7, 3))
 
 
 def tile_list_speckle_energy_kernel(
@@ -34,7 +34,8 @@ def tile_list_speckle_energy_kernel(
     out_0, out_1, out_2, out_3,
 ):
     nc = tc.nc
-    y_tiles = len(PIECES) * ROW_TILES
+    y_tiles = PIECES * ROW_TILES
+    twice = (PIECES - 1, 0)
     with ExitStack() as ctx:
         keep = ctx.enter_context(tc.tile_pool(name="keep", bufs=1))
         work = ctx.enter_context(tc.tile_pool(name="work", bufs=1))
@@ -62,16 +63,16 @@ def tile_list_speckle_energy_kernel(
         nc.scalar.activation(warm[:], one[:], ACT.Abs_reciprocal_sqrt)
 
         def load_planes(planes, scales):
-            for quad in range(QUADS):
+            for s in range(4):
                 nc.sync.dma_start(
-                    planes[32 * quad : 32 * quad + 4, :].bitcast(I32).rearrange("s (a c) -> s a c", a=PASSES),
-                    scales[:, 4 * quad : 4 * quad + 4, :].rearrange("a s c -> s a c").bitcast(I32),
+                    planes[s:P:32, :].bitcast(I32).rearrange("q (a c) -> q a c", a=PASSES),
+                    scales[:, s:16:4, :].rearrange("a q c -> q a c").bitcast(I32),
                 )
 
         w1_rows = w1.rearrange("(a p i) c -> a p i c", p=P, i=PACK)
         tab_rows = tab_words.rearrange("a p t i -> a p (t i)").bitcast(I32)
         w1_raw0 = held("weight_buffer", [P, PACK, H], F32)
-        w1_raw1 = held("w1_raw1", [P, PACK, H], F32)
+        w1_raw1 = [held("w1_raw1%d" % c, [P, PACK, H // 2], F32) for c in range(2)]
         tab_w0 = held("tab_w0", [P, T], U32)
         w2_w_raw = held("w2_w_raw", [P, PASSES, 2 * H], U8)
         gain_t = held("gain_t", [P, PACK], F32)
@@ -94,20 +95,20 @@ def tile_list_speckle_energy_kernel(
         nc.vector.tensor_copy(picked_s[:], tab_s[:].indirect(offsets[:]))
 
         def move_plane(a):
-            for quad in range(QUADS):
-                first = 4 * (16 * a + 4 * quad)
+            for s in range(4):
+                first = 4 * (16 * a + s)
                 nc.sync.dma_start(
-                    v_planes[a][32 * quad : 32 * quad + 4, :].bitcast(I32),
-                    picked_s[first : first + 13 : 4, :].bitcast(I32),
+                    v_planes[a][s:P:32, :].bitcast(I32), picked_s[first : first + 49 : 16, :].bitcast(I32)
                 )
 
         move_plane(0)
         tab_w1 = held("table_buffer", [P, T], U32)
         nc.sync.dma_start(tab_w1[:].bitcast(I32), tab_rows[1])
         move_plane(1)
-        nc.sync.dma_start(w1_raw1[:], w1_rows[1])
+        for c in range(2):
+            nc.sync.dma_start(w1_raw1[c][:], w1_rows[1][:, :, c * H // 2 : (c + 1) * H // 2])
         nc.sync.dma_start(gain_t[:], gain.rearrange("(p t) -> p t", t=PACK))
-        w4_raw = held("weight_buffer", [P, PACK, N], F32)
+        w4_raw = held("w4_raw", [P, PACK, N], F32)
         w3_w = held("w3_w", [P, PASSES, N], U32)
         nc.sync.dma_start(w4_raw[:], w4.rearrange("(p i) n -> p i n", i=PACK))
         nc.sync.dma_start(w3_w[:].bitcast(I32), w3_words.rearrange("a p n i -> p a (n i)").bitcast(I32))
@@ -131,28 +132,40 @@ def tile_list_speckle_energy_kernel(
                 entries = offsets[:, u * HALF // 16 : (u + 1) * HALF // 16]
                 nc.vector.tensor_copy(v_w[a][u][:], tab_w[:].indirect(entries))
 
-        w1_bf1 = [held("w1_bf1%d" % pair, [P, 2 * P * PACK], BF16) for pair in range(2)]
-        for pair, copy in enumerate((nc.vector.tensor_copy, nc.scalar.copy)):
+        def round_w1(c, pair, copy):
+            rounded = held("w1_bf1%d%d" % (c, pair), [P, 2, P // 2 * PACK], BF16)
             copy(
-                w1_bf1[pair][:].rearrange("p (t m i) -> p m t i", t=2, i=PACK),
-                w1_raw1[:].rearrange("p i (m t) -> p m t i", t=PACK)[:, :, 2 * pair : 2 * pair + 2],
+                rounded[:].rearrange("p t (m i) -> p m t i", i=PACK),
+                w1_raw1[c][:].rearrange("p i (m t) -> p m t i", t=PACK)[:, :, 2 * pair : 2 * pair + 2],
             )
-        for pair in range(2):
-            cols = slice(2 * pair * P, 2 * (pair + 1) * P)
-            nc.vector.quantize_mx(out=w1_w[:, 1, cols].bitcast(FP8X4), scales=w1_s[:, 1, cols], in_=w1_bf1[pair][:])
+            return rounded
 
-        w4_bf = held("w4_bf", [P, N * PACK], BF16)
+        def quantise_w1(c, pair, rounded):
+            for t in range(2 * pair, 2 * pair + 2):
+                cols = slice(t * P + c * P // 2, t * P + (c + 1) * P // 2)
+                nc.vector.quantize_mx(
+                    out=w1_w[:, 1, cols].bitcast(FP8X4), scales=w1_s[:, 1, cols], in_=rounded[:, t % 2, :]
+                )
+
+        early = [round_w1(0, pair, nc.scalar.copy) for pair in range(2)]
+        late = [round_w1(1, pair, copy) for pair, copy in enumerate((nc.vector.tensor_copy, nc.scalar.copy))]
+        for pair in range(2):
+            quantise_w1(0, pair, early[pair])
+            quantise_w1(1, pair, late[pair])
+
         w4_w = held("w4_w", [P, N], U32)
         w4_s = held("w4_s", [P, N], U8)
+        w4_bf = held("w4_bf", [P, N * PACK], BF16)
+        nc.gpsimd.tensor_scalar(
+            w4_bf[:].rearrange("p (c i) -> p c i", i=PACK), w4_raw[:].rearrange("p i c -> p c i"),
+            1.0, 0.0, ALU.mult, ALU.add,
+        )
 
-        def quantise_w4(n):
-            cols = slice(n * P, (n + 1) * P)
-            wide = slice(n * P * PACK, (n + 1) * P * PACK)
-            nc.scalar.copy(
-                w4_bf[:, wide].rearrange("p (c e i) -> p c i e", e=4, i=PACK),
-                w4_raw[:, :, cols].rearrange("p i (c e) -> p c i e", e=4),
+        def quantise_w4(index):
+            first, end = ((0, 2 * P), (2 * P, N))[index]
+            nc.vector.quantize_mx(
+                out=w4_w[:, first:end].bitcast(FP8X4), scales=w4_s[:, first:end], in_=w4_bf[:, first * PACK : end * PACK]
             )
-            nc.vector.quantize_mx(out=w4_w[:, cols].bitcast(FP8X4), scales=w4_s[:, cols], in_=w4_bf[:, wide])
 
         def pass_over_v(out, a, words, scales, first, width):
             u, inner = divmod(first, HALF)
@@ -172,8 +185,8 @@ def tile_list_speckle_energy_kernel(
             pass_over_v(w2_bank[:], a, words, w2_s[:, a, t * P : (t + 1) * P], u * HALF, HALF)
 
         h = [held("h%d" % u, [P, PACK, HALF], F32) for u in range(HALVES)]
-        h_bf = [held("h_bf%d" % k, [P, width * PACK], BF16) for k, (first, width) in enumerate(PIECES)]
-        h_w = [held("h_w%d" % k, [P, width], U32) for k, (first, width) in enumerate(PIECES)]
+        h_bf = [held("h_bf%d" % k, [P, PIECE * PACK], BF16) for k in range(PIECES)]
+        h_w = [held("h_w%d" % u, [P, HALF], U32) for u in range(HALVES)]
         h_s = held("h_s", [P, S], U8)
         h_rows = out_1.rearrange("(p t) j -> p t j", t=PACK)
         h_codes = out_2[0].rearrange("p m i -> p (m i)").bitcast(I32)
@@ -191,57 +204,63 @@ def tile_list_speckle_energy_kernel(
         def store_h(u):
             nc.sync.dma_start(h_rows[:, :, u * HALF : (u + 1) * HALF], h[u][:])
 
-        def round_h(k):
-            first, width = PIECES[k]
-            u, inner = divmod(first, HALF)
-            nc.vector.tensor_copy(
-                h_bf[k][:].rearrange("p (c e t) -> p c t e", e=4, t=PACK),
+        def round_h(k, copy, first=0, width=PIECE):
+            u, inner = divmod(k * PIECE + first, HALF)
+            copy(
+                h_bf[k][:, first * PACK : (first + width) * PACK].rearrange("p (c e t) -> p c t e", e=4, t=PACK),
                 h[u][:, :, inner : inner + width].rearrange("p t (c e) -> p c t e", e=4),
             )
 
+        def h_piece(k):
+            u, inner = divmod(k * PIECE, HALF)
+            return h_w[u][:, inner : inner + PIECE].bitcast(FP8X4), h_s[:, k * PIECE : (k + 1) * PIECE]
+
         def quantise_h(k):
-            first, width = PIECES[k]
-            cols = slice(first, first + width)
-            nc.vector.quantize_mx(out=h_w[k][:].bitcast(FP8X4), scales=h_s[:, cols], in_=h_bf[k][:])
-            nc.sync.dma_start(h_codes[:, cols], h_w[k][:].bitcast(I32))
+            words, scales = h_piece(k)
+            nc.vector.quantize_mx(out=words, scales=scales, in_=h_bf[k][:])
+
+        def store_codes(u):
+            nc.sync.dma_start(h_codes[:, u * HALF : (u + 1) * HALF], h_w[u][:].bitcast(I32))
 
         def scalar_squares(k, n):
-            place = k * ROW_TILES + n
-            return place < SCALAR_SQUARES or place >= y_tiles - SCALAR_SQUARES
+            return (k, n) not in BY_GPSIMD and (k, n) != twice
 
-        def products(k, n):
-            first, width = PIECES[k]
+        def response(k, n):
             rows = slice(n * P, (n + 1) * P)
-            banks = [bank(index) for index in BANKS[k][n]]
-            q_sum = banks[0][:, :width]
-            c_sum = banks[-1][:, HALF - width :]
-            for a in range(PASSES):
-                scales = w3_s[:, a * N + n * P : a * N + (n + 1) * P]
-                pass_over_v(c_sum, a, w3_w[:, a, rows].bitcast(FP8X4), scales, first, width)
+            words, scales = h_piece(k)
+            q_sum = psum.tile([P, PIECE], F32, name="bank%d" % n)
             nc.tensor.matmul_mx(
-                out=q_sum, lhsT=w4_w[:, rows].bitcast(FP8X4), lhsT_scale=w4_s[:, rows],
-                rhs=h_w[k][:].bitcast(FP8X4), rhs_scale=h_s[:, first : first + width], start=True, stop=True,
+                out=q_sum[:], lhsT=w4_w[:, rows].bitcast(FP8X4), lhsT_scale=w4_s[:, rows],
+                rhs=words, rhs_scale=scales, start=True, stop=True,
             )
-            magnitude = work.tile([P, width], F32, name="magnitude", bufs=ROW_TILES)
-            root = work.tile([P, width], F32, name="root", bufs=y_tiles)
-            nc.scalar.activation(magnitude[:], q_sum, ACT.Abs)
+            magnitude = work.tile([P, PIECE], F32, name="magnitude", bufs=ROW_TILES)
+            root = work.tile([P, PIECE], F32, name="root", bufs=y_tiles)
+            nc.scalar.activation(magnitude[:], q_sum[:], ACT.Abs)
             nc.scalar.activation(root[:], magnitude[:], ACT.Abs_reciprocal_sqrt, bias=1.0)
             if scalar_squares(k, n):
-                inverse = work.tile([P, width], F32, name="inverse", bufs=2 * SCALAR_SQUARES)
+                inverse = work.tile([P, PIECE], F32, name="inverse", bufs=y_tiles - len(BY_GPSIMD) - 1)
                 nc.scalar.activation(inverse[:], root[:], ACT.Square)
-                return c_sum, inverse
-            return c_sum, root
+                return inverse[:]
+            return root[:]
+
+        def direct(u, n):
+            c_sum = bank(C_BANKS[u][n])
+            for a in range(PASSES):
+                scales = w3_s[:, a * N + n * P : a * N + (n + 1) * P]
+                pass_over_v(c_sum[:], a, w3_w[:, a, n * P : (n + 1) * P].bitcast(FP8X4), scales, u * HALF, HALF)
+            return c_sum
 
         def finish(k, n, c_sum, factor):
-            first, width = PIECES[k]
-            y = work.tile([P, width], F32, name="y", bufs=y_tiles)
-            if scalar_squares(k, n):
-                nc.vector.tensor_tensor(y[:], c_sum, factor[:], ALU.mult)
+            inner = k * PIECE % HALF
+            c_part = c_sum[:, inner : inner + PIECE]
+            y = work.tile([P, PIECE], F32, name="y", bufs=y_tiles)
+            if (k, n) != twice:
+                nc.vector.tensor_tensor(y[:], c_part, factor, ALU.mult)
             else:
-                once = work.tile([P, width], F32, name="once", bufs=y_tiles - 2 * SCALAR_SQUARES)
-                nc.vector.tensor_tensor(once[:], c_sum, factor[:], ALU.mult)
-                nc.vector.tensor_tensor(y[:], once[:], factor[:], ALU.mult)
-            nc.sync.dma_start(out_0[n * P : (n + 1) * P, first : first + width], y[:])
+                once = held("once", [P, PIECE], F32)
+                nc.vector.tensor_tensor(once[:], c_part, factor, ALU.mult)
+                nc.vector.tensor_tensor(y[:], once[:], factor, ALU.mult)
+            nc.sync.dma_start(out_0[n * P : (n + 1) * P, k * PIECE : (k + 1) * PIECE], y[:])
 
         w1_banks = [bank(t) for t in range(PACK)]
         w2_banks = [bank(PACK + t) for t in range(PACK)]
@@ -254,9 +273,6 @@ def tile_list_speckle_energy_kernel(
             w1_pass(w1_banks[t], 1, t, 0)
             combine(square(w1_banks[t]), w2_banks[t], t, 0)
         store_h(0)
-        round_h(0)
-        quantise_w4(0)
-        quantise_h(0)
 
         def w1_squared(t):
             w1_bank = bank(t)
@@ -264,39 +280,53 @@ def tile_list_speckle_energy_kernel(
                 w1_pass(w1_bank, a, t, 1)
             return square(w1_bank)
 
-        def w2_product(t):
+        def second_half(t):
             w2_bank = bank(PACK + t)
             for a in range(PASSES):
                 w2_pass(w2_bank, a, t, 1)
-            return w2_bank
+            combine(squares[t], w2_bank, t, 1)
 
-        squares = []
-        w2_sums = []
-        for pair in range(2):
-            squares.extend([w1_squared(2 * pair), w1_squared(2 * pair + 1)])
-            w2_sums.append(w2_product(pair))
+        squares = [w1_squared(t) for t in range(PACK)]
+        round_h(0, nc.vector.tensor_copy)
+        round_h(1, nc.scalar.copy, 0, PIECE // 2)
+        quantise_w4(0)
+        quantise_h(0)
+        factors = {(0, n): response(0, n) for n in range(2)}
+        round_h(1, nc.vector.tensor_copy, PIECE // 2, PIECE // 2)
+        second_half(0)
         quantise_w4(1)
-        pending = {(0, n): products(0, n) for n in range(2)}
-        w2_sums.extend([w2_product(2), w2_product(3)])
-        for t in range(PACK):
-            combine(squares[t], w2_sums[t], t, 1)
-        quantise_w4(2)
-        pending[0, 2] = products(0, 2)
-        store_h(1)
-        round_h(1)
-        round_h(2)
+        factors[0, 2] = response(0, 2)
         quantise_h(1)
-        quantise_h(2)
-
+        store_codes(0)
         for n in range(ROW_TILES):
-            pending[1, n] = products(1, n)
-        for n in range(ROW_TILES - 1):
-            pending[2, n] = products(2, n)
-        finish(0, 0, *pending[0, 0])
-        pending[2, ROW_TILES - 1] = products(2, ROW_TILES - 1)
-        for quad in range(QUADS):
-            nc.sync.dma_start(
-                out_3[0, 4 * quad : 4 * quad + 4, :].bitcast(I32), h_s[32 * quad : 32 * quad + 4, :].bitcast(I32)
-            )
-        for k, n in sorted(pending)[1:]:
-            finish(k, n, *pending[k, n])
+            factors[1, n] = response(1, n)
+        for t in range(1, PACK):
+            second_half(t)
+        store_h(1)
+        sums = {(0, n): direct(0, n) for n in range(ROW_TILES)}
+        finish(0, 0, sums[0, 0], factors[0, 0])
+        round_h(2, nc.vector.tensor_copy)
+        finish(0, 1, sums[0, 1], factors[0, 1])
+        quantise_h(2)
+        for n in range(ROW_TILES):
+            factors[2, n] = response(2, n)
+        round_h(3, nc.vector.tensor_copy)
+        finish(0, 2, sums[0, 2], factors[0, 2])
+        quantise_h(3)
+        late_squares = held("h_bf%d" % (PIECES - 1), [P, len(BY_GPSIMD), PIECE], F32)
+        for place, (k, n) in enumerate(BY_GPSIMD):
+            nc.gpsimd.tensor_tensor(late_squares[:, place, :], factors[k, n], factors[k, n], ALU.mult)
+            factors[k, n] = late_squares[:, place, :]
+        store_codes(1)
+        for n in range(ROW_TILES):
+            factors[3, n] = response(3, n)
+        for s in range(4):
+            nc.sync.dma_start(out_3[0, s:16:4, :].bitcast(I32), h_s[s:P:32, :].bitcast(I32))
+        for n in (2, 0, 1):
+            finish(1, n, sums[0, n], factors[1, n])
+        for n in range(ROW_TILES):
+            sums[1, n] = direct(1, n)
+        for n in (0, 2, 1):
+            finish(2, n, sums[1, n], factors[2, n])
+        for n in range(ROW_TILES):
+            finish(3, n, sums[1, n], factors[3, n])

@@ -107,10 +107,13 @@ def tile_list_speckle_energy_kernel(
         move_plane(1)
         for c in range(2):
             nc.sync.dma_start(w1_raw1[c][:], w1_rows[1][:, :, c * H // 2 : (c + 1) * H // 2])
-        nc.sync.dma_start(gain_t[:], gain.rearrange("(p t) -> p t", t=PACK))
-        w4_raw = held("w4_raw", [P, PACK, N], F32)
+        w4_first = held("w4_first", [P, PACK, P], F32)
+        w4_rest = held("w4_rest", [P, PACK, N - P], F32)
+        w4_rows = w4.rearrange("(p i) n -> p i n", i=PACK)
         w3_w = held("w3_w", [P, PASSES, N], U32)
-        nc.sync.dma_start(w4_raw[:], w4.rearrange("(p i) n -> p i n", i=PACK))
+        nc.sync.dma_start(w4_first[:], w4_rows[:, :, :P])
+        nc.sync.dma_start(gain_t[:], gain.rearrange("(p t) -> p t", t=PACK))
+        nc.sync.dma_start(w4_rest[:], w4_rows[:, :, P:])
         nc.sync.dma_start(w3_w[:].bitcast(I32), w3_words.rearrange("a p n i -> p a (n i)").bitcast(I32))
         load_planes(w3_s, w3_scales)
 
@@ -132,32 +135,33 @@ def tile_list_speckle_energy_kernel(
                 entries = offsets[:, u * HALF // 16 : (u + 1) * HALF // 16]
                 nc.vector.tensor_copy(v_w[a][u][:], tab_w[:].indirect(entries))
 
+        w1_bf1 = [held("w1_bf1%d" % pair, [P, 2, P * PACK], BF16) for pair in range(2)]
+
         def round_w1(c, pair, copy):
-            rounded = held("w1_bf1%d%d" % (c, pair), [P, 2, P // 2 * PACK], BF16)
             copy(
-                rounded[:].rearrange("p t (m i) -> p m t i", i=PACK),
+                w1_bf1[pair][:, :, c * P * 2 : (c + 1) * P * 2].rearrange("p t (m i) -> p m t i", i=PACK),
                 w1_raw1[c][:].rearrange("p i (m t) -> p m t i", t=PACK)[:, :, 2 * pair : 2 * pair + 2],
             )
-            return rounded
 
-        def quantise_w1(c, pair, rounded):
-            for t in range(2 * pair, 2 * pair + 2):
-                cols = slice(t * P + c * P // 2, t * P + (c + 1) * P // 2)
-                nc.vector.quantize_mx(
-                    out=w1_w[:, 1, cols].bitcast(FP8X4), scales=w1_s[:, 1, cols], in_=rounded[:, t % 2, :]
-                )
-
-        early = [round_w1(0, pair, nc.scalar.copy) for pair in range(2)]
-        late = [round_w1(1, pair, copy) for pair, copy in enumerate((nc.vector.tensor_copy, nc.scalar.copy))]
-        for pair in range(2):
-            quantise_w1(0, pair, early[pair])
-            quantise_w1(1, pair, late[pair])
+        round_w1(0, 0, nc.scalar.copy)
+        round_w1(0, 1, nc.scalar.copy)
+        round_w1(1, 0, nc.vector.tensor_copy)
+        round_w1(1, 1, nc.scalar.copy)
+        for t in range(PACK):
+            cols = slice(t * P, (t + 1) * P)
+            nc.vector.quantize_mx(
+                out=w1_w[:, 1, cols].bitcast(FP8X4), scales=w1_s[:, 1, cols], in_=w1_bf1[t // 2][:, t % 2, :]
+            )
 
         w4_w = held("w4_w", [P, N], U32)
         w4_s = held("w4_s", [P, N], U8)
         w4_bf = held("w4_bf", [P, N * PACK], BF16)
+        nc.vector.tensor_copy(
+            w4_bf[:, : P * PACK].rearrange("p (c e i) -> p c i e", e=4, i=PACK),
+            w4_first[:].rearrange("p i (c e) -> p c i e", e=4),
+        )
         nc.gpsimd.tensor_scalar(
-            w4_bf[:].rearrange("p (c i) -> p c i", i=PACK), w4_raw[:].rearrange("p i c -> p c i"),
+            w4_bf[:, P * PACK :].rearrange("p (c i) -> p c i", i=PACK), w4_rest[:].rearrange("p i c -> p c i"),
             1.0, 0.0, ALU.mult, ALU.add,
         )
 

@@ -25,7 +25,7 @@ ROW_TILES = N // P
 
 PIECE = HALF // 2
 PIECES = S // PIECE
-BY_GPSIMD = ((1, 0), (1, 1), (2, 0), (2, 1))
+GPSIMD_TILES = 2
 C_BANKS = ((3, 4, 5), (6, 7, 3))
 
 
@@ -35,7 +35,6 @@ def tile_list_speckle_energy_kernel(
 ):
     nc = tc.nc
     y_tiles = PIECES * ROW_TILES
-    twice = (PIECES - 1, 0)
     with ExitStack() as ctx:
         keep = ctx.enter_context(tc.tile_pool(name="keep", bufs=1))
         work = ctx.enter_context(tc.tile_pool(name="work", bufs=1))
@@ -155,21 +154,17 @@ def tile_list_speckle_energy_kernel(
 
         w4_w = held("w4_w", [P, N], U32)
         w4_s = held("w4_s", [P, N], U8)
-        w4_bf = held("w4_bf", [P, N * PACK], BF16)
+        first_bf = held("w4_bf", [P, P * PACK], BF16)
         nc.vector.tensor_copy(
-            w4_bf[:, : P * PACK].rearrange("p (c e i) -> p c i e", e=4, i=PACK),
+            first_bf[:].rearrange("p (c e i) -> p c i e", e=4, i=PACK),
             w4_first[:].rearrange("p i (c e) -> p c i e", e=4),
         )
+        nc.vector.quantize_mx(out=w4_w[:, :P].bitcast(FP8X4), scales=w4_s[:, :P], in_=first_bf[:])
+        rest_bf = held("w4_bf", [P, (N - P) * PACK], BF16)
         nc.gpsimd.tensor_scalar(
-            w4_bf[:, P * PACK :].rearrange("p (c i) -> p c i", i=PACK), w4_rest[:].rearrange("p i c -> p c i"),
+            rest_bf[:].rearrange("p (c i) -> p c i", i=PACK), w4_rest[:].rearrange("p i c -> p c i"),
             1.0, 0.0, ALU.mult, ALU.add,
         )
-
-        def quantise_w4(index):
-            first, end = ((0, 2 * P), (2 * P, N))[index]
-            nc.vector.quantize_mx(
-                out=w4_w[:, first:end].bitcast(FP8X4), scales=w4_s[:, first:end], in_=w4_bf[:, first * PACK : end * PACK]
-            )
 
         def pass_over_v(out, a, words, scales, first, width):
             u, inner = divmod(first, HALF)
@@ -227,7 +222,7 @@ def tile_list_speckle_energy_kernel(
             nc.sync.dma_start(h_codes[:, u * HALF : (u + 1) * HALF], h_w[u][:].bitcast(I32))
 
         def scalar_squares(k, n):
-            return (k, n) not in BY_GPSIMD and (k, n) != twice
+            return n >= GPSIMD_TILES or k == PIECES - 1
 
         def response(k, n):
             rows = slice(n * P, (n + 1) * P)
@@ -242,10 +237,17 @@ def tile_list_speckle_energy_kernel(
             nc.scalar.activation(magnitude[:], q_sum[:], ACT.Abs)
             nc.scalar.activation(root[:], magnitude[:], ACT.Abs_reciprocal_sqrt, bias=1.0)
             if scalar_squares(k, n):
-                inverse = work.tile([P, PIECE], F32, name="inverse", bufs=y_tiles - len(BY_GPSIMD) - 1)
+                inverse = work.tile([P, PIECE], F32, name="inverse", bufs=y_tiles - GPSIMD_TILES * (PIECES - 1))
                 nc.scalar.activation(inverse[:], root[:], ACT.Square)
                 return inverse[:]
             return root[:]
+
+        def square_on_gpsimd(pieces, behind):
+            squares = held("h_bf%d" % behind, [P, len(pieces), GPSIMD_TILES, PIECE], F32)
+            for place, k in enumerate(pieces):
+                for n in range(GPSIMD_TILES):
+                    nc.gpsimd.tensor_tensor(squares[:, place, n, :], factors[k, n], factors[k, n], ALU.mult)
+                    factors[k, n] = squares[:, place, n, :]
 
         def direct(u, n):
             c_sum = bank(C_BANKS[u][n])
@@ -258,12 +260,7 @@ def tile_list_speckle_energy_kernel(
             inner = k * PIECE % HALF
             c_part = c_sum[:, inner : inner + PIECE]
             y = work.tile([P, PIECE], F32, name="y", bufs=y_tiles)
-            if (k, n) != twice:
-                nc.vector.tensor_tensor(y[:], c_part, factor, ALU.mult)
-            else:
-                once = held("once", [P, PIECE], F32)
-                nc.vector.tensor_tensor(once[:], c_part, factor, ALU.mult)
-                nc.vector.tensor_tensor(y[:], once[:], factor, ALU.mult)
+            nc.vector.tensor_tensor(y[:], c_part, factor, ALU.mult)
             nc.sync.dma_start(out_0[n * P : (n + 1) * P, k * PIECE : (k + 1) * PIECE], y[:])
 
         w1_banks = [bank(t) for t in range(PACK)]
@@ -293,14 +290,13 @@ def tile_list_speckle_energy_kernel(
         squares = [w1_squared(t) for t in range(PACK)]
         round_h(0, nc.vector.tensor_copy)
         round_h(1, nc.scalar.copy, 0, PIECE // 2)
-        quantise_w4(0)
+        nc.vector.quantize_mx(out=w4_w[:, P:].bitcast(FP8X4), scales=w4_s[:, P:], in_=rest_bf[:])
         quantise_h(0)
-        factors = {(0, n): response(0, n) for n in range(2)}
+        factors = {(0, n): response(0, n) for n in range(ROW_TILES)}
         round_h(1, nc.vector.tensor_copy, PIECE // 2, PIECE // 2)
         second_half(0)
-        quantise_w4(1)
-        factors[0, 2] = response(0, 2)
         quantise_h(1)
+        square_on_gpsimd((0,), 1)
         store_codes(0)
         for n in range(ROW_TILES):
             factors[1, n] = response(1, n)
@@ -317,10 +313,7 @@ def tile_list_speckle_energy_kernel(
         round_h(3, nc.vector.tensor_copy)
         finish(0, 2, sums[0, 2], factors[0, 2])
         quantise_h(3)
-        late_squares = held("h_bf%d" % (PIECES - 1), [P, len(BY_GPSIMD), PIECE], F32)
-        for place, (k, n) in enumerate(BY_GPSIMD):
-            nc.gpsimd.tensor_tensor(late_squares[:, place, :], factors[k, n], factors[k, n], ALU.mult)
-            factors[k, n] = late_squares[:, place, :]
+        square_on_gpsimd((1, 2), 3)
         store_codes(1)
         for n in range(ROW_TILES):
             factors[3, n] = response(3, n)

@@ -25,7 +25,7 @@ ROW_TILES = N // P
 
 PIECE = HALF // 2
 PIECES = S // PIECE
-GPSIMD_TILES = 2
+BY_GPSIMD = ((1, 0), (1, 1), (2, 0), (2, 1))
 C_BANKS = ((3, 4, 5), (6, 7, 3))
 
 
@@ -35,6 +35,7 @@ def tile_list_speckle_energy_kernel(
 ):
     nc = tc.nc
     y_tiles = PIECES * ROW_TILES
+    twice = (PIECES - 1, 0)
     with ExitStack() as ctx:
         keep = ctx.enter_context(tc.tile_pool(name="keep", bufs=1))
         work = ctx.enter_context(tc.tile_pool(name="work", bufs=1))
@@ -222,7 +223,7 @@ def tile_list_speckle_energy_kernel(
             nc.sync.dma_start(h_codes[:, u * HALF : (u + 1) * HALF], h_w[u][:].bitcast(I32))
 
         def scalar_squares(k, n):
-            return n >= GPSIMD_TILES or k == PIECES - 1
+            return (k, n) not in BY_GPSIMD and (k, n) != twice
 
         def response(k, n):
             rows = slice(n * P, (n + 1) * P)
@@ -237,17 +238,10 @@ def tile_list_speckle_energy_kernel(
             nc.scalar.activation(magnitude[:], q_sum[:], ACT.Abs)
             nc.scalar.activation(root[:], magnitude[:], ACT.Abs_reciprocal_sqrt, bias=1.0)
             if scalar_squares(k, n):
-                inverse = work.tile([P, PIECE], F32, name="inverse", bufs=y_tiles - GPSIMD_TILES * (PIECES - 1))
+                inverse = work.tile([P, PIECE], F32, name="inverse", bufs=y_tiles - len(BY_GPSIMD) - 1)
                 nc.scalar.activation(inverse[:], root[:], ACT.Square)
                 return inverse[:]
             return root[:]
-
-        def square_on_gpsimd(pieces, behind):
-            squares = held("h_bf%d" % behind, [P, len(pieces), GPSIMD_TILES, PIECE], F32)
-            for place, k in enumerate(pieces):
-                for n in range(GPSIMD_TILES):
-                    nc.gpsimd.tensor_tensor(squares[:, place, n, :], factors[k, n], factors[k, n], ALU.mult)
-                    factors[k, n] = squares[:, place, n, :]
 
         def direct(u, n):
             c_sum = bank(C_BANKS[u][n])
@@ -260,7 +254,12 @@ def tile_list_speckle_energy_kernel(
             inner = k * PIECE % HALF
             c_part = c_sum[:, inner : inner + PIECE]
             y = work.tile([P, PIECE], F32, name="y", bufs=y_tiles)
-            nc.vector.tensor_tensor(y[:], c_part, factor, ALU.mult)
+            if (k, n) != twice:
+                nc.vector.tensor_tensor(y[:], c_part, factor, ALU.mult)
+            else:
+                once = held("once", [P, PIECE], F32)
+                nc.vector.tensor_tensor(once[:], c_part, factor, ALU.mult)
+                nc.vector.tensor_tensor(y[:], once[:], factor, ALU.mult)
             nc.sync.dma_start(out_0[n * P : (n + 1) * P, k * PIECE : (k + 1) * PIECE], y[:])
 
         w1_banks = [bank(t) for t in range(PACK)]
@@ -296,7 +295,6 @@ def tile_list_speckle_energy_kernel(
         round_h(1, nc.vector.tensor_copy, PIECE // 2, PIECE // 2)
         second_half(0)
         quantise_h(1)
-        square_on_gpsimd((0,), 1)
         store_codes(0)
         for n in range(ROW_TILES):
             factors[1, n] = response(1, n)
@@ -313,7 +311,10 @@ def tile_list_speckle_energy_kernel(
         round_h(3, nc.vector.tensor_copy)
         finish(0, 2, sums[0, 2], factors[0, 2])
         quantise_h(3)
-        square_on_gpsimd((1, 2), 3)
+        late_squares = held("h_bf%d" % (PIECES - 1), [P, len(BY_GPSIMD), PIECE], F32)
+        for place, (k, n) in enumerate(BY_GPSIMD):
+            nc.gpsimd.tensor_tensor(late_squares[:, place, :], factors[k, n], factors[k, n], ALU.mult)
+            factors[k, n] = late_squares[:, place, :]
         store_codes(1)
         for n in range(ROW_TILES):
             factors[3, n] = response(3, n)

@@ -87,8 +87,8 @@ def tile_list_speckle_energy_kernel(
         w1_s = held("w1_s", [P, PASSES, H], U8)
         w1_bf0 = held("w1_bf0", [P, H * PACK], BF16)
         nc.scalar.copy(
-            w1_bf0[:].rearrange("p (t m i) -> p m t i", t=PACK, i=PACK),
-            w1_raw0[:].rearrange("p i (m t) -> p m t i", t=PACK),
+            w1_bf0[:].rearrange("p (t m i) -> p m i t", t=PACK, i=PACK),
+            w1_raw0[:].rearrange("p i (m t) -> p m i t", t=PACK),
         )
 
         picked_s = held("picked_s", [P, S], U8)
@@ -139,8 +139,8 @@ def tile_list_speckle_energy_kernel(
 
         def round_w1(c, pair, copy):
             copy(
-                w1_bf1[pair][:, :, c * P * 2 : (c + 1) * P * 2].rearrange("p t (m i) -> p m t i", i=PACK),
-                w1_raw1[c][:].rearrange("p i (m t) -> p m t i", t=PACK)[:, :, 2 * pair : 2 * pair + 2],
+                w1_bf1[pair][:, :, c * P * 2 : (c + 1) * P * 2].rearrange("p t (m i) -> p m i t", i=PACK),
+                w1_raw1[c][:].rearrange("p i (m t) -> p m i t", t=PACK)[:, :, :, 2 * pair : 2 * pair + 2],
             )
 
         round_w1(0, 0, nc.scalar.copy)

@@ -25,8 +25,10 @@ ROW_TILES = N // P
 
 PIECE = HALF // 2
 PIECES = S // PIECE
-BY_GPSIMD = ((1, 0), (1, 1), (2, 0), (2, 1))
-C_BANKS = ((3, 4, 5), (6, 7, 3))
+TWICE = ((1, 0), (1, 1), (1, 2), (2, 0), (2, 1), (2, 2), (3, 0))
+SECOND_W2_BANKS = (4, 5, 2, 3)
+Q_BANKS = (6, 7, 0, 1)
+C_BANKS = ((4, 5, 2), (3, 4, 5))
 
 
 def tile_list_speckle_energy_kernel(
@@ -35,7 +37,6 @@ def tile_list_speckle_energy_kernel(
 ):
     nc = tc.nc
     y_tiles = PIECES * ROW_TILES
-    twice = (PIECES - 1, 0)
     with ExitStack() as ctx:
         keep = ctx.enter_context(tc.tile_pool(name="keep", bufs=1))
         work = ctx.enter_context(tc.tile_pool(name="work", bufs=1))
@@ -185,7 +186,7 @@ def tile_list_speckle_energy_kernel(
             pass_over_v(w2_bank[:], a, words, w2_s[:, a, t * P : (t + 1) * P], u * HALF, HALF)
 
         h = [held("h%d" % u, [P, PACK, HALF], F32) for u in range(HALVES)]
-        h_bf = [held("h_bf%d" % k, [P, PIECE * PACK], BF16) for k in range(PIECES)]
+        h_bf = {}
         h_w = [held("h_w%d" % u, [P, HALF], U32) for u in range(HALVES)]
         h_s = held("h_s", [P, S], U8)
         h_rows = out_1.rearrange("(p t) j -> p t j", t=PACK)
@@ -204,31 +205,44 @@ def tile_list_speckle_energy_kernel(
         def store_h(u):
             nc.sync.dma_start(h_rows[:, :, u * HALF : (u + 1) * HALF], h[u][:])
 
-        def round_h(k, copy, first=0, width=PIECE):
-            u, inner = divmod(k * PIECE + first, HALF)
-            copy(
-                h_bf[k][:, first * PACK : (first + width) * PACK].rearrange("p (c e t) -> p c t e", e=4, t=PACK),
-                h[u][:, :, inner : inner + width].rearrange("p t (c e) -> p c t e", e=4),
-            )
+        def round_h(k, parts=1):
+            u, inner = divmod(k * PIECE, HALF)
+            h_bf[k] = held("h_bf%d" % u, [P, PIECE * PACK], BF16)
+            source = h[u][:, :, inner : inner + PIECE]
+            if inner == 0:
+                width = PIECE // parts
+                for first in range(0, PIECE, width):
+                    nc.vector.tensor_copy(
+                        h_bf[k][:, first * PACK : (first + width) * PACK].rearrange("p (c e t) -> p c t e", e=4, t=PACK),
+                        source[:, :, first : first + width].rearrange("p t (c e) -> p c t e", e=4),
+                    )
+            else:
+                nc.gpsimd.tensor_scalar(
+                    h_bf[k][:].rearrange("p (c t) -> p c t", t=PACK), source.rearrange("p t c -> p c t"),
+                    1.0, 0.0, ALU.mult, ALU.add,
+                )
 
         def h_piece(k):
             u, inner = divmod(k * PIECE, HALF)
             return h_w[u][:, inner : inner + PIECE].bitcast(FP8X4), h_s[:, k * PIECE : (k + 1) * PIECE]
 
-        def quantise_h(k):
-            words, scales = h_piece(k)
-            nc.vector.quantize_mx(out=words, scales=scales, in_=h_bf[k][:])
+        def quantise_h(k, parts=1):
+            u, inner = divmod(k * PIECE, HALF)
+            width = PIECE // parts
+            for first in range(0, PIECE, width):
+                nc.vector.quantize_mx(
+                    out=h_w[u][:, inner + first : inner + first + width].bitcast(FP8X4),
+                    scales=h_s[:, k * PIECE + first : k * PIECE + first + width],
+                    in_=h_bf[k][:, first * PACK : (first + width) * PACK],
+                )
 
         def store_codes(u):
             nc.sync.dma_start(h_codes[:, u * HALF : (u + 1) * HALF], h_w[u][:].bitcast(I32))
 
-        def scalar_squares(k, n):
-            return (k, n) not in BY_GPSIMD and (k, n) != twice
-
         def response(k, n):
             rows = slice(n * P, (n + 1) * P)
             words, scales = h_piece(k)
-            q_sum = psum.tile([P, PIECE], F32, name="bank%d" % n)
+            q_sum = psum.tile([P, PIECE], F32, name="bank%d" % Q_BANKS[(k * ROW_TILES + n) % len(Q_BANKS)])
             nc.tensor.matmul_mx(
                 out=q_sum[:], lhsT=w4_w[:, rows].bitcast(FP8X4), lhsT_scale=w4_s[:, rows],
                 rhs=words, rhs_scale=scales, start=True, stop=True,
@@ -237,8 +251,8 @@ def tile_list_speckle_energy_kernel(
             root = work.tile([P, PIECE], F32, name="root", bufs=y_tiles)
             nc.scalar.activation(magnitude[:], q_sum[:], ACT.Abs)
             nc.scalar.activation(root[:], magnitude[:], ACT.Abs_reciprocal_sqrt, bias=1.0)
-            if scalar_squares(k, n):
-                inverse = work.tile([P, PIECE], F32, name="inverse", bufs=y_tiles - len(BY_GPSIMD) - 1)
+            if (k, n) not in TWICE:
+                inverse = work.tile([P, PIECE], F32, name="inverse", bufs=y_tiles - len(TWICE))
                 nc.scalar.activation(inverse[:], root[:], ACT.Square)
                 return inverse[:]
             return root[:]
@@ -250,17 +264,14 @@ def tile_list_speckle_energy_kernel(
                 pass_over_v(c_sum[:], a, w3_w[:, a, n * P : (n + 1) * P].bitcast(FP8X4), scales, u * HALF, HALF)
             return c_sum
 
-        def finish(k, n, c_sum, factor):
+        def times_c(k, n, name):
             inner = k * PIECE % HALF
-            c_part = c_sum[:, inner : inner + PIECE]
-            y = work.tile([P, PIECE], F32, name="y", bufs=y_tiles)
-            if (k, n) != twice:
-                nc.vector.tensor_tensor(y[:], c_part, factor, ALU.mult)
-            else:
-                once = held("once", [P, PIECE], F32)
-                nc.vector.tensor_tensor(once[:], c_part, factor, ALU.mult)
-                nc.vector.tensor_tensor(y[:], once[:], factor, ALU.mult)
-            nc.sync.dma_start(out_0[n * P : (n + 1) * P, k * PIECE : (k + 1) * PIECE], y[:])
+            product = work.tile([P, PIECE], F32, name=name, bufs=len(TWICE))
+            nc.vector.tensor_tensor(product[:], sums[k * PIECE // HALF, n][:, inner : inner + PIECE], factors[k, n], ALU.mult)
+            return product[:]
+
+        def store_y(k, n, y):
+            nc.sync.dma_start(out_0[n * P : (n + 1) * P, k * PIECE : (k + 1) * PIECE], y)
 
         w1_banks = [bank(t) for t in range(PACK)]
         w2_banks = [bank(PACK + t) for t in range(PACK)]
@@ -281,50 +292,57 @@ def tile_list_speckle_energy_kernel(
             return square(w1_bank)
 
         def second_half(t):
-            w2_bank = bank(PACK + t)
+            w2_bank = bank(SECOND_W2_BANKS[t])
             for a in range(PASSES):
                 w2_pass(w2_bank, a, t, 1)
             combine(squares[t], w2_bank, t, 1)
 
         squares = [w1_squared(t) for t in range(PACK)]
-        round_h(0, nc.vector.tensor_copy)
-        round_h(1, nc.scalar.copy, 0, PIECE // 2)
         nc.vector.quantize_mx(out=w4_w[:, P:].bitcast(FP8X4), scales=w4_s[:, P:], in_=rest_bf[:])
-        quantise_h(0)
+        round_h(0, 2)
+        quantise_h(0, 2)
         factors = {(0, n): response(0, n) for n in range(ROW_TILES)}
-        round_h(1, nc.vector.tensor_copy, PIECE // 2, PIECE // 2)
-        second_half(0)
+        round_h(1)
+        for t in range(PACK - 1):
+            second_half(t)
         quantise_h(1)
         store_codes(0)
         for n in range(ROW_TILES):
             factors[1, n] = response(1, n)
-        for t in range(1, PACK):
-            second_half(t)
+        second_half(PACK - 1)
         store_h(1)
         sums = {(0, n): direct(0, n) for n in range(ROW_TILES)}
-        finish(0, 0, sums[0, 0], factors[0, 0])
-        round_h(2, nc.vector.tensor_copy)
-        finish(0, 1, sums[0, 1], factors[0, 1])
+        round_h(2)
+        store_y(0, 0, times_c(0, 0, "y"))
         quantise_h(2)
         for n in range(ROW_TILES):
             factors[2, n] = response(2, n)
-        round_h(3, nc.vector.tensor_copy)
-        finish(0, 2, sums[0, 2], factors[0, 2])
+        round_h(3)
+        for n in range(1, ROW_TILES):
+            store_y(0, n, times_c(0, n, "y"))
+        once = {(1, n): times_c(1, n, "once") for n in range(ROW_TILES)}
         quantise_h(3)
-        late_squares = held("h_bf%d" % (PIECES - 1), [P, len(BY_GPSIMD), PIECE], F32)
-        for place, (k, n) in enumerate(BY_GPSIMD):
-            nc.gpsimd.tensor_tensor(late_squares[:, place, :], factors[k, n], factors[k, n], ALU.mult)
-            factors[k, n] = late_squares[:, place, :]
         store_codes(1)
         for n in range(ROW_TILES):
             factors[3, n] = response(3, n)
         for s in range(4):
             nc.sync.dma_start(out_3[0, s:16:4, :].bitcast(I32), h_s[s:P:32, :].bitcast(I32))
-        for n in (2, 0, 1):
-            finish(1, n, sums[0, n], factors[1, n])
+        late_y = held("h_bf%d" % (HALVES - 1), [P, len(TWICE), PIECE], F32)
+
+        def again(k, n):
+            y = late_y[:, TWICE.index((k, n)), :]
+            nc.vector.tensor_tensor(y, once[k, n], factors[k, n], ALU.mult)
+            store_y(k, n, y)
+
+        for n in range(ROW_TILES):
+            again(1, n)
         for n in range(ROW_TILES):
             sums[1, n] = direct(1, n)
-        for n in (0, 2, 1):
-            finish(2, n, sums[1, n], factors[2, n])
         for n in range(ROW_TILES):
-            finish(3, n, sums[1, n], factors[3, n])
+            once[2, n] = times_c(2, n, "once")
+        for n in range(ROW_TILES):
+            again(2, n)
+        once[3, 0] = times_c(3, 0, "once")
+        again(3, 0)
+        for n in range(1, ROW_TILES):
+            store_y(3, n, times_c(3, n, "y"))

@@ -164,7 +164,8 @@ def tile_list_speckle_energy_kernel(
         nc.vector.quantize_mx(out=w4_w[:, :P].bitcast(FP8X4), scales=w4_s[:, :P], in_=first_bf[:])
         rest_bf = held("w4_bf", [P, (N - P) * PACK], BF16)
         nc.gpsimd.tensor_scalar(
-            rest_bf[:].rearrange("p (c i) -> p c i", i=PACK), w4_rest[:].rearrange("p i c -> p c i"),
+            rest_bf[:].rearrange("p (c e i) -> p c i e", e=2, i=PACK),
+            w4_rest[:].rearrange("p i (c e) -> p c i e", e=2),
             1.0, 0.0, ALU.mult, ALU.add,
         )
 
@@ -218,7 +219,8 @@ def tile_list_speckle_energy_kernel(
                     )
             else:
                 nc.gpsimd.tensor_scalar(
-                    h_bf[k][:].rearrange("p (c t) -> p c t", t=PACK), source.rearrange("p t c -> p c t"),
+                    h_bf[k][:].rearrange("p (c e t) -> p c t e", e=2, t=PACK),
+                    source.rearrange("p t (c e) -> p c t e", e=2),
                     1.0, 0.0, ALU.mult, ALU.add,
                 )
 

@@ -43,12 +43,12 @@ def tile_list_speckle_energy_kernel(
         psum = ctx.enter_context(tc.psum_pool(name="psum", bufs=1))
 
         def held(name, shape, dtype):
-            return keep.tile(shape, dtype, name=name, align_bytes=64)
+            return keep.tile(shape, dtype, name=name, align_bytes=256)
 
         def bank(index):
             return psum.tile([P, HALF], F32, name="bank%d" % index)
 
-        offsets = keep.tile([P, S // 16], U16, name="offsets")
+        offsets = keep.tile([P, S // 16], U16, name="offsets", align_bytes=256)
         tab_s = held("table_buffer", [P, T], U8)
         w2_s_raw = held("w2_s_raw", [P, PASSES * H], U8)
         w3_s = held("w3_s", [P, PASSES * N], U8)
@@ -194,7 +194,7 @@ def tile_list_speckle_energy_kernel(
         h_codes = out_2[0].rearrange("p m i -> p (m i)").bitcast(I32)
 
         def square(w1_bank):
-            squared = work.tile([P, HALF], F32, name="squared", bufs=PACK + 1)
+            squared = work.tile([P, HALF], F32, name="squared", bufs=PACK + 1, align_bytes=256)
             nc.scalar.activation(squared[:], w1_bank[:], ACT.Square)
             return squared
 
@@ -249,12 +249,12 @@ def tile_list_speckle_energy_kernel(
                 out=q_sum[:], lhsT=w4_w[:, rows].bitcast(FP8X4), lhsT_scale=w4_s[:, rows],
                 rhs=words, rhs_scale=scales, start=True, stop=True,
             )
-            magnitude = work.tile([P, PIECE], F32, name="magnitude", bufs=ROW_TILES)
-            root = work.tile([P, PIECE], F32, name="root", bufs=y_tiles)
+            magnitude = work.tile([P, PIECE], F32, name="magnitude", bufs=ROW_TILES, align_bytes=256)
+            root = work.tile([P, PIECE], F32, name="root", bufs=y_tiles, align_bytes=256)
             nc.scalar.activation(magnitude[:], q_sum[:], ACT.Abs)
             nc.scalar.activation(root[:], magnitude[:], ACT.Abs_reciprocal_sqrt, bias=1.0)
             if (k, n) not in TWICE:
-                inverse = work.tile([P, PIECE], F32, name="inverse", bufs=y_tiles - len(TWICE))
+                inverse = work.tile([P, PIECE], F32, name="inverse", bufs=y_tiles - len(TWICE), align_bytes=256)
                 nc.scalar.activation(inverse[:], root[:], ACT.Square)
                 return inverse[:]
             return root[:]
@@ -268,7 +268,7 @@ def tile_list_speckle_energy_kernel(
 
         def times_c(k, n, name):
             inner = k * PIECE % HALF
-            product = work.tile([P, PIECE], F32, name=name, bufs=len(TWICE))
+            product = work.tile([P, PIECE], F32, name=name, bufs=len(TWICE), align_bytes=256)
             nc.vector.tensor_tensor(product[:], sums[k * PIECE // HALF, n][:, inner : inner + PIECE], factors[k, n], ALU.mult)
             return product[:]
 

@@ -25,10 +25,13 @@ ROW_TILES = N // P
 
 PIECE = HALF // 2
 PIECES = S // PIECE
-TWICE = ((1, 0), (1, 1), (1, 2), (2, 0), (2, 1), (2, 2), (3, 0))
+TWICE = ((0, 2), (1, 0), (1, 1), (1, 2), (2, 0), (2, 1), (2, 2), (3, 0))
 SECOND_W2_BANKS = (4, 5, 2, 3)
-Q_BANKS = (6, 7, 0, 1)
-C_BANKS = ((4, 5, 2), (3, 4, 5))
+Q_BANKS = ((6, 7, 0), (1, 2, 6), (7, 0, 2), (6, 7, 0))
+C_BANKS = ((4, 5, 3), (1, 4, 5))
+LINE = 256
+SCALE_ROWS_AT = 4 * T - LINE
+ROUNDED_AT = 7 * T
 
 
 def tile_list_speckle_energy_kernel(
@@ -39,32 +42,34 @@ def tile_list_speckle_energy_kernel(
     y_tiles = PIECES * ROW_TILES
     with ExitStack() as ctx:
         keep = ctx.enter_context(tc.tile_pool(name="keep", bufs=1))
+        staged = ctx.enter_context(tc.tile_pool(name="staged", bufs=1))
         work = ctx.enter_context(tc.tile_pool(name="work", bufs=1))
         psum = ctx.enter_context(tc.psum_pool(name="psum", bufs=1))
 
         def held(name, shape, dtype):
             return keep.tile(shape, dtype, name=name, align_bytes=256)
 
+        def placed(name, shape, dtype, offset):
+            return staged.tile(shape, dtype, name=name, align_bytes=LINE, offset=offset)
+
         def bank(index):
             return psum.tile([P, HALF], F32, name="bank%d" % index)
 
         offsets = keep.tile([P, S // 16], U16, name="offsets", align_bytes=256)
-        tab_s = held("table_buffer", [P, T], U8)
+        tab_s = placed("tab_s", [P, T], U8, SCALE_ROWS_AT)
         w2_s_raw = held("w2_s_raw", [P, PASSES * H], U8)
-        w3_s = held("w3_s", [P, PASSES * N], U8)
         v_planes = [held("v_plane%d" % a, [P, S], U8) for a in range(PASSES)]
         nc.vector.memset(tab_s[:].bitcast(I32), 0)
         one = held("one", [P, 1], F32)
         nc.vector.memset(one[:], 1.0)
         nc.vector.memset(w2_s_raw[:].bitcast(I32), 0)
-        nc.vector.memset(w3_s[:].bitcast(I32), 0)
         for plane in v_planes:
             nc.vector.memset(plane[:].bitcast(I32), 0)
         warm = held("warm", [P, 1], F32)
         nc.scalar.activation(warm[:], one[:], ACT.Abs_reciprocal_sqrt)
 
-        def load_planes(planes, scales):
-            for s in range(4):
+        def load_planes(planes, scales, rows):
+            for s in rows:
                 nc.sync.dma_start(
                     planes[s:P:32, :].bitcast(I32).rearrange("q (a c) -> q a c", a=PASSES),
                     scales[:, s:16:4, :].rearrange("a q c -> q a c").bitcast(I32),
@@ -72,25 +77,24 @@ def tile_list_speckle_energy_kernel(
 
         w1_rows = w1.rearrange("(a p i) c -> a p i c", p=P, i=PACK)
         tab_rows = tab_words.rearrange("a p t i -> a p (t i)").bitcast(I32)
-        w1_raw0 = held("weight_buffer", [P, PACK, H], F32)
-        w1_raw1 = [held("w1_raw1%d" % c, [P, PACK, H // 2], F32) for c in range(2)]
+        w1_parts = (slice(0, PACK - 1), slice(PACK - 1, PACK))
+        w1_raw0 = [held("w1_raw0%d" % j, [P, rows.stop - rows.start, H], F32) for j, rows in enumerate(w1_parts)]
         tab_w0 = held("tab_w0", [P, T], U32)
-        w2_w_raw = held("w2_w_raw", [P, PASSES, 2 * H], U8)
-        gain_t = held("gain_t", [P, PACK], F32)
-        nc.sync.dma_start(w1_raw0[:], w1_rows[0])
+        nc.sync.dma_start(w1_raw0[0][:], w1_rows[0][:, w1_parts[0], :])
         nc.sync.dma_start(tab_s[0:P:4, :].bitcast(I32), tab_scales.rearrange("a q t -> (a q) t").bitcast(I32))
         nc.sync.dma_start(offsets[:], offs)
-        load_planes(w2_s_raw, w2_scales)
+        load_planes(w2_s_raw, w2_scales, range(4))
         nc.sync.dma_start(tab_w0[:].bitcast(I32), tab_rows[0])
-        nc.sync.dma_start(w2_w_raw[:].bitcast(I32), w2_words.rearrange("a p c -> p a c").bitcast(I32))
+        nc.sync.dma_start(w1_raw0[1][:], w1_rows[0][:, w1_parts[1], :])
 
         w1_w = held("w1_w", [P, PASSES, H], U32)
         w1_s = held("w1_s", [P, PASSES, H], U8)
-        w1_bf0 = held("w1_bf0", [P, H * PACK], BF16)
-        nc.scalar.copy(
-            w1_bf0[:].rearrange("p (t m i) -> p m i t", t=PACK, i=PACK),
-            w1_raw0[:].rearrange("p i (m t) -> p m i t", t=PACK),
-        )
+        w1_bf0 = placed("w1_bf0", [P, H * PACK], BF16, ROUNDED_AT)
+        for j in range(2):
+            nc.scalar.copy(
+                w1_bf0[:].rearrange("p (t m i) -> p m i t", t=PACK, i=PACK)[:, :, w1_parts[j], :],
+                w1_raw0[j][:].rearrange("p i (m t) -> p m i t", t=PACK),
+            )
 
         picked_s = held("picked_s", [P, S], U8)
         nc.vector.tensor_copy(picked_s[:], tab_s[:].indirect(offsets[:]))
@@ -103,32 +107,44 @@ def tile_list_speckle_energy_kernel(
                 )
 
         move_plane(0)
-        tab_w1 = held("table_buffer", [P, T], U32)
+        tab_w1 = placed("tab_w1", [P, T], U32, 0)
         nc.sync.dma_start(tab_w1[:].bitcast(I32), tab_rows[1])
         move_plane(1)
-        for c in range(2):
-            nc.sync.dma_start(w1_raw1[c][:], w1_rows[1][:, :, c * H // 2 : (c + 1) * H // 2])
-        w4_first = held("w4_first", [P, PACK, P], F32)
-        w4_rest = held("w4_rest", [P, PACK, N - P], F32)
-        w4_rows = w4.rearrange("(p i) n -> p i n", i=PACK)
-        w3_w = held("w3_w", [P, PASSES, N], U32)
-        nc.sync.dma_start(w4_first[:], w4_rows[:, :, :P])
-        nc.sync.dma_start(gain_t[:], gain.rearrange("(p t) -> p t", t=PACK))
-        nc.sync.dma_start(w4_rest[:], w4_rows[:, :, P:])
-        nc.sync.dma_start(w3_w[:].bitcast(I32), w3_words.rearrange("a p n i -> p a (n i)").bitcast(I32))
-        load_planes(w3_s, w3_scales)
+        w2_w_raw = placed("w2_w_raw", [P, PASSES, 2 * H], U8, 4 * T + LINE)
+        nc.sync.dma_start(w2_w_raw[:].bitcast(I32), w2_words.rearrange("a p c -> p a c").bitcast(I32))
+        w1_flat1 = placed("w1_raw1", [P, PACK * H], F32, SCALE_ROWS_AT + T - LINE)
+        w1_cols = (slice(0, H // 2), slice(H // 2, 3 * H // 4), slice(3 * H // 4, H))
+        w1_raw1 = [
+            w1_flat1[:, PACK * cols.start : PACK * cols.stop].rearrange("p (i c) -> p i c", i=PACK) for cols in w1_cols
+        ]
+        for part, cols in zip(w1_raw1, w1_cols):
+            nc.sync.dma_start(part, w1_rows[1][:, :, cols])
 
         w2_w = held("w2_w", [P, PASSES, 2 * H], U8)
-        w2_s = held("w2_s", [P, PASSES, H], U8)
+        w2_s = placed("w2_s", [P, PASSES, H], U8, 4 * T + LINE + 4 * H)
         nc.vector.tensor_copy(
             w2_s[:].rearrange("p a (t m) -> p a t m", t=PACK),
             w2_s_raw[:].rearrange("p (a m t) -> p a t m", a=PASSES, t=PACK),
         )
-        nc.vector.tensor_copy(
-            w2_w[:].rearrange("p a (t m b) -> p a t m b", t=PACK, b=2),
-            w2_w_raw[:].rearrange("p a (m t b) -> p a t m b", t=PACK, b=2),
-        )
+        for a in range(PASSES):
+            nc.scalar.copy(
+                w2_w[:, a, :].bitcast(U16).rearrange("p (t m) -> p m t", t=PACK),
+                w2_w_raw[:, a, :].bitcast(U16).rearrange("p (m t) -> p m t", t=PACK),
+            )
         nc.vector.quantize_mx(out=w1_w[:, 0, :].bitcast(FP8X4), scales=w1_s[:, 0, :], in_=w1_bf0[:])
+
+        gain_t = placed("gain_t", [P, PACK], F32, 4 * T)
+        w4_first = placed("w4_first", [P, PACK, P], F32, ROUNDED_AT)
+        w3_s = placed("w3_s", [P, PASSES * N], U8, ROUNDED_AT + 4 * PACK * P)
+        w4_rest = held("w1_raw01", [P, PACK, N - P], F32)
+        w3_w = held("w1_raw00", [P, PASSES, N], U32)
+        w4_rows = w4.rearrange("(p i) n -> p i n", i=PACK)
+        nc.vector.memset(w3_s[:].bitcast(I32), 0)
+        nc.sync.dma_start(w4_first[:], w4_rows[:, :, :P])
+        nc.sync.dma_start(gain_t[:], gain.rearrange("(p t) -> p t", t=PACK))
+        nc.sync.dma_start(w4_rest[:], w4_rows[:, :, P:])
+        nc.sync.dma_start(w3_w[:].bitcast(I32), w3_words.rearrange("a p n i -> p a (n i)").bitcast(I32))
+        load_planes(w3_s, w3_scales, range(4))
 
         v_w = [[held("v_w%d%d" % (a, u), [P, HALF], U32) for u in range(HALVES)] for a in range(PASSES)]
         for a, tab_w in enumerate((tab_w0, tab_w1)):
@@ -140,14 +156,16 @@ def tile_list_speckle_energy_kernel(
 
         def round_w1(c, pair, copy):
             copy(
-                w1_bf1[pair][:, :, c * P * 2 : (c + 1) * P * 2].rearrange("p t (m i) -> p m i t", i=PACK),
-                w1_raw1[c][:].rearrange("p i (m t) -> p m i t", t=PACK)[:, :, :, 2 * pair : 2 * pair + 2],
+                w1_bf1[pair][:, :, w1_cols[c]].rearrange("p t (m i) -> p m i t", i=PACK),
+                w1_raw1[c].rearrange("p i (m t) -> p m i t", t=PACK)[:, :, :, 2 * pair : 2 * pair + 2],
             )
 
         round_w1(0, 0, nc.scalar.copy)
         round_w1(0, 1, nc.scalar.copy)
         round_w1(1, 0, nc.vector.tensor_copy)
-        round_w1(1, 1, nc.scalar.copy)
+        round_w1(1, 1, nc.vector.tensor_copy)
+        round_w1(2, 0, nc.vector.tensor_copy)
+        round_w1(2, 1, nc.scalar.copy)
         for t in range(PACK):
             cols = slice(t * P, (t + 1) * P)
             nc.vector.quantize_mx(
@@ -244,7 +262,7 @@ def tile_list_speckle_energy_kernel(
         def response(k, n):
             rows = slice(n * P, (n + 1) * P)
             words, scales = h_piece(k)
-            q_sum = psum.tile([P, PIECE], F32, name="bank%d" % Q_BANKS[(k * ROW_TILES + n) % len(Q_BANKS)])
+            q_sum = psum.tile([P, PIECE], F32, name="bank%d" % Q_BANKS[k][n])
             nc.tensor.matmul_mx(
                 out=q_sum[:], lhsT=w4_w[:, rows].bitcast(FP8X4), lhsT_scale=w4_s[:, rows],
                 rhs=words, rhs_scale=scales, start=True, stop=True,
@@ -266,11 +284,14 @@ def tile_list_speckle_energy_kernel(
                 pass_over_v(c_sum[:], a, w3_w[:, a, n * P : (n + 1) * P].bitcast(FP8X4), scales, u * HALF, HALF)
             return c_sum
 
-        def times_c(k, n, name):
+        def times_c(k, n, product):
             inner = k * PIECE % HALF
-            product = work.tile([P, PIECE], F32, name=name, bufs=len(TWICE), align_bytes=256)
-            nc.vector.tensor_tensor(product[:], sums[k * PIECE // HALF, n][:, inner : inner + PIECE], factors[k, n], ALU.mult)
+            c_part = sums[k * PIECE // HALF, n][:, inner : inner + PIECE]
+            nc.vector.tensor_tensor(product[:], c_part, factors[k, n], ALU.mult)
             return product[:]
+
+        def y_tile():
+            return work.tile([P, PIECE], F32, name="y", bufs=y_tiles - len(TWICE), align_bytes=256)
 
         def store_y(k, n, y):
             nc.sync.dma_start(out_0[n * P : (n + 1) * P, k * PIECE : (k + 1) * PIECE], y)
@@ -305,46 +326,53 @@ def tile_list_speckle_energy_kernel(
         quantise_h(0, 2)
         factors = {(0, n): response(0, n) for n in range(ROW_TILES)}
         round_h(1)
-        for t in range(PACK - 1):
+        for t in range(PACK):
             second_half(t)
+        store_h(1)
         quantise_h(1)
         store_codes(0)
         for n in range(ROW_TILES):
             factors[1, n] = response(1, n)
-        second_half(PACK - 1)
-        store_h(1)
         sums = {(0, n): direct(0, n) for n in range(ROW_TILES)}
-        round_h(2)
-        store_y(0, 0, times_c(0, 0, "y"))
-        quantise_h(2)
+        round_h(2, 2)
+        quantise_h(2, 2)
         for n in range(ROW_TILES):
             factors[2, n] = response(2, n)
         round_h(3)
-        for n in range(1, ROW_TILES):
-            store_y(0, n, times_c(0, n, "y"))
-        once = {(1, n): times_c(1, n, "once") for n in range(ROW_TILES)}
+        pair = held("pair", [P, 2, PIECE], F32)
+        for n in range(ROW_TILES - 1):
+            times_c(0, n, pair[:, n, :])
+        nc.sync.dma_start(out_0[: 2 * P, :PIECE].rearrange("(n p) j -> p n j", p=P), pair[:])
+        once = {}
+
+        def first_product(k, n):
+            once[k, n] = times_c(k, n, held("once%d%d" % (k, n), [P, PIECE], F32))
+
+        def second_product(k, n, y, engine=nc.vector):
+            engine.tensor_tensor(y, once[k, n], factors[k, n], ALU.mult)
+            store_y(k, n, y)
+
+        for k, n in TWICE[: 1 + ROW_TILES]:
+            first_product(k, n)
         quantise_h(3)
         store_codes(1)
         for n in range(ROW_TILES):
             factors[3, n] = response(3, n)
         for s in range(4):
             nc.sync.dma_start(out_3[0, s:16:4, :].bitcast(I32), h_s[s:P:32, :].bitcast(I32))
-        late_y = held("h_bf%d" % (HALVES - 1), [P, len(TWICE), PIECE], F32)
-
-        def again(k, n):
-            y = late_y[:, TWICE.index((k, n)), :]
-            nc.vector.tensor_tensor(y, once[k, n], factors[k, n], ALU.mult)
-            store_y(k, n, y)
-
-        for n in range(ROW_TILES):
-            again(1, n)
+        early_y = held("h_bf%d" % (HALVES - 1), [P, ROW_TILES, PIECE], F32)
+        second_product(0, 2, early_y[:, 0, :])
+        for n in range(2):
+            nc.vector.tensor_tensor(early_y[:, 1 + n, :], once[1, n], factors[1, n], ALU.mult)
+        nc.sync.dma_start(out_0[: 2 * P, PIECE : 2 * PIECE].rearrange("(n p) j -> p n j", p=P), early_y[:, 1:, :])
+        second_product(1, 2, held("once11", [P, PIECE], F32)[:], nc.gpsimd)
         for n in range(ROW_TILES):
             sums[1, n] = direct(1, n)
-        for n in range(ROW_TILES):
-            once[2, n] = times_c(2, n, "once")
-        for n in range(ROW_TILES):
-            again(2, n)
-        once[3, 0] = times_c(3, 0, "once")
-        again(3, 0)
+        late_tiles = TWICE[1 + ROW_TILES :]
+        for k, n in late_tiles:
+            first_product(k, n)
+        late_y = held("once12", [P, len(late_tiles), PIECE], F32)
+        for place, (k, n) in enumerate(late_tiles):
+            second_product(k, n, late_y[:, place, :])
         for n in range(1, ROW_TILES):
-            store_y(3, n, times_c(3, n, "y"))
+            store_y(3, n, times_c(3, n, y_tile()))

@@ -113,7 +113,7 @@ def tile_list_speckle_energy_kernel(
         w2_w_raw = placed("w2_w_raw", [P, PASSES, 2 * H], U8, 4 * T + LINE)
         nc.sync.dma_start(w2_w_raw[:].bitcast(I32), w2_words.rearrange("a p c -> p a c").bitcast(I32))
         w1_flat1 = placed("w1_raw1", [P, PACK * H], F32, SCALE_ROWS_AT + T - LINE)
-        w1_cols = (slice(0, H // 2), slice(H // 2, 3 * H // 4), slice(3 * H // 4, H))
+        w1_cols = (slice(0, 3 * H // 4), slice(3 * H // 4, H))
         w1_raw1 = [
             w1_flat1[:, PACK * cols.start : PACK * cols.stop].rearrange("p (i c) -> p i c", i=PACK) for cols in w1_cols
         ]
@@ -160,12 +160,9 @@ def tile_list_speckle_energy_kernel(
                 w1_raw1[c].rearrange("p i (m t) -> p m i t", t=PACK)[:, :, :, 2 * pair : 2 * pair + 2],
             )
 
-        round_w1(0, 0, nc.scalar.copy)
-        round_w1(0, 1, nc.scalar.copy)
-        round_w1(1, 0, nc.vector.tensor_copy)
-        round_w1(1, 1, nc.vector.tensor_copy)
-        round_w1(2, 0, nc.vector.tensor_copy)
-        round_w1(2, 1, nc.scalar.copy)
+        for c in range(2):
+            round_w1(c, 0, nc.vector.tensor_copy)
+            round_w1(c, 1, nc.scalar.copy)
         for t in range(PACK):
             cols = slice(t * P, (t + 1) * P)
             nc.vector.quantize_mx(
@@ -306,7 +303,8 @@ def tile_list_speckle_energy_kernel(
         for t in range(PACK):
             w1_pass(w1_banks[t], 1, t, 0)
             combine(square(w1_banks[t]), w2_banks[t], t, 0)
-        store_h(0)
+        for pair in (slice(0, 2), slice(2, PACK)):
+            nc.sync.dma_start(h_rows[:, pair, :HALF], h[0][:, pair, :])
 
         def w1_squared(t):
             w1_bank = bank(t)

from contextlib import ExitStack

import concourse.mybir as mybir

K, T, S, H, N = 1024, 4096, 1024, 512, 384
FLOPS = 2 * S * (2 * K * H + K * N + H * N)

F32 = mybir.dt.float32
BF16 = mybir.dt.bfloat16
I32 = mybir.dt.int32
U32 = mybir.dt.uint32
U16 = mybir.dt.uint16
U8 = mybir.dt.uint8
FP8X4 = mybir.dt.float8_e4m3fn_x4
FP4X4 = mybir.dt.float4_e2m1fn_x4
ACT = mybir.ActivationFunctionType
ALU = mybir.AluOpType

P = 128
PACK = 4
PASSES = K // (P * PACK)
HALF = 512
HALVES = S // HALF
ROW_TILES = N // P

PIECE = HALF // 2
PIECES = S // PIECE
TWICE = ((0, 2), (1, 0), (1, 1), (1, 2), (2, 0), (2, 1), (2, 2), (3, 0))
SECOND_W2_BANKS = (4, 5, 2, 3)
Q_BANKS = ((6, 7, 0), (1, 2, 6), (7, 0, 2), (6, 7, 0))
C_BANKS = ((4, 5, 3), (1, 4, 5))
LINE = 256
SCALE_ROWS_AT = 4 * T - LINE
ROUNDED_AT = 7 * T


def tile_list_speckle_energy_kernel(
    tc, tab_words, tab_scales, offs, w1, gain, w2_words, w2_scales, w3_words, w3_scales, w4,
    out_0, out_1, out_2, out_3,
):
    nc = tc.nc
    y_tiles = PIECES * ROW_TILES
    with ExitStack() as ctx:
        keep = ctx.enter_context(tc.tile_pool(name="keep", bufs=1))
        staged = ctx.enter_context(tc.tile_pool(name="staged", bufs=1))
        work = ctx.enter_context(tc.tile_pool(name="work", bufs=1))
        psum = ctx.enter_context(tc.psum_pool(name="psum", bufs=1))

        def held(name, shape, dtype):
            return keep.tile(shape, dtype, name=name, align_bytes=256)

        def placed(name, shape, dtype, offset):
            return staged.tile(shape, dtype, name=name, align_bytes=LINE, offset=offset)

        def bank(index):
            return psum.tile([P, HALF], F32, name="bank%d" % index)

        offsets = keep.tile([P, S // 16], U16, name="offsets", align_bytes=256)
        tab_s = placed("tab_s", [P, T], U8, SCALE_ROWS_AT)
        w2_s_raw = held("w2_s_raw", [P, PASSES * H], U8)
        v_planes = [held("v_plane%d" % a, [P, S], U8) for a in range(PASSES)]
        nc.vector.memset(tab_s[:].bitcast(I32), 0)
        one = held("one", [P, 1], F32)
        nc.vector.memset(one[:], 1.0)
        nc.vector.memset(w2_s_raw[:].bitcast(I32), 0)
        for plane in v_planes:
            nc.vector.memset(plane[:].bitcast(I32), 0)
        warm = held("warm", [P, 1], F32)
        nc.scalar.activation(warm[:], one[:], ACT.Abs_reciprocal_sqrt)

        def load_planes(planes, scales, rows):
            for s in rows:
                nc.sync.dma_start(
                    planes[s:P:32, :].bitcast(I32).rearrange("q (a c) -> q a c", a=PASSES),
                    scales[:, s:16:4, :].rearrange("a q c -> q a c").bitcast(I32),
                )

        w1_rows = w1.rearrange("(a p i) c -> a p i c", p=P, i=PACK)
        tab_rows = tab_words.rearrange("a p t i -> a p (t i)").bitcast(I32)
        w1_parts = (slice(0, PACK - 1), slice(PACK - 1, PACK))
        w1_raw0 = [held("w1_raw0%d" % j, [P, rows.stop - rows.start, H], F32) for j, rows in enumerate(w1_parts)]
        tab_w0 = held("tab_w0", [P, T], U32)
        nc.sync.dma_start(w1_raw0[0][:], w1_rows[0][:, w1_parts[0], :])
        nc.sync.dma_start(tab_s[0:P:4, :].bitcast(I32), tab_scales.rearrange("a q t -> (a q) t").bitcast(I32))
        nc.sync.dma_start(offsets[:], offs)
        load_planes(w2_s_raw, w2_scales, range(4))
        nc.sync.dma_start(tab_w0[:].bitcast(I32), tab_rows[0])
        nc.sync.dma_start(w1_raw0[1][:], w1_rows[0][:, w1_parts[1], :])

        w1_w = held("w1_w", [P, PASSES, H], U32)
        w1_s = held("w1_s", [P, PASSES, H], U8)
        w1_bf0 = placed("w1_bf0", [P, H * PACK], BF16, ROUNDED_AT)
        for j in range(2):
            nc.scalar.copy(
                w1_bf0[:].rearrange("p (t m i) -> p m i t", t=PACK, i=PACK)[:, :, w1_parts[j], :],
                w1_raw0[j][:].rearrange("p i (m t) -> p m i t", t=PACK),
            )

        picked_s = held("picked_s", [P, S], U8)
        nc.vector.tensor_copy(picked_s[:], tab_s[:].indirect(offsets[:]))

        def move_plane(a):
            for s in range(4):
                first = 4 * (16 * a + s)
                nc.sync.dma_start(
                    v_planes[a][s:P:32, :].bitcast(I32), picked_s[first : first + 49 : 16, :].bitcast(I32)
                )

        move_plane(0)
        tab_w1 = placed("tab_w1", [P, T], U32, 0)
        nc.sync.dma_start(tab_w1[:].bitcast(I32), tab_rows[1])
        move_plane(1)
        w2_w_raw = placed("w2_w_raw", [P, PASSES, 2 * H], U8, 4 * T + LINE)
        nc.sync.dma_start(w2_w_raw[:].bitcast(I32), w2_words.rearrange("a p c -> p a c").bitcast(I32))
        w1_flat1 = placed("w1_raw1", [P, PACK * H], F32, SCALE_ROWS_AT + T - LINE)
        w1_cols = (slice(0, 3 * H // 4), slice(3 * H // 4, H))
        w1_raw1 = [
            w1_flat1[:, PACK * cols.start : PACK * cols.stop].rearrange("p (i c) -> p i c", i=PACK) for cols in w1_cols
        ]
        for part, cols in zip(w1_raw1, w1_cols):
            nc.sync.dma_start(part, w1_rows[1][:, :, cols])

        w2_w = held("w2_w", [P, PASSES, 2 * H], U8)
        w2_s = placed("w2_s", [P, PASSES, H], U8, 4 * T + LINE + 4 * H)
        nc.vector.tensor_copy(
            w2_s[:].rearrange("p a (t m) -> p a t m", t=PACK),
            w2_s_raw[:].rearrange("p (a m t) -> p a t m", a=PASSES, t=PACK),
        )
        for a in range(PASSES):
            nc.scalar.copy(
                w2_w[:, a, :].bitcast(U16).rearrange("p (t m) -> p m t", t=PACK),
                w2_w_raw[:, a, :].bitcast(U16).rearrange("p (m t) -> p m t", t=PACK),
            )
        nc.vector.quantize_mx(out=w1_w[:, 0, :].bitcast(FP8X4), scales=w1_s[:, 0, :], in_=w1_bf0[:])

        gain_t = placed("gain_t", [P, PACK], F32, 4 * T)
        w4_first = placed("w4_first", [P, PACK, P], F32, ROUNDED_AT)
        w3_s = placed("w3_s", [P, PASSES * N], U8, ROUNDED_AT + 4 * PACK * P)
        w4_rest = held("w1_raw01", [P, PACK, N - P], F32)
        w3_w = held("w1_raw00", [P, PASSES, N], U32)
        w4_rows = w4.rearrange("(p i) n -> p i n", i=PACK)
        nc.vector.memset(w3_s[:].bitcast(I32), 0)
        nc.sync.dma_start(w4_first[:], w4_rows[:, :, :P])
        nc.sync.dma_start(gain_t[:], gain.rearrange("(p t) -> p t", t=PACK))
        nc.sync.dma_start(w4_rest[:], w4_rows[:, :, P:])
        nc.sync.dma_start(w3_w[:].bitcast(I32), w3_words.rearrange("a p n i -> p a (n i)").bitcast(I32))
        load_planes(w3_s, w3_scales, range(4))

        v_w = [[held("v_w%d%d" % (a, u), [P, HALF], U32) for u in range(HALVES)] for a in range(PASSES)]
        for a, tab_w in enumerate((tab_w0, tab_w1)):
            for u in range(HALVES):
                entries = offsets[:, u * HALF // 16 : (u + 1) * HALF // 16]
                nc.vector.tensor_copy(v_w[a][u][:], tab_w[:].indirect(entries))

        w1_bf1 = [held("w1_bf1%d" % pair, [P, 2, P * PACK], BF16) for pair in range(2)]

        def round_w1(c, pair, copy):
            copy(
                w1_bf1[pair][:, :, w1_cols[c]].rearrange("p t (m i) -> p m i t", i=PACK),
                w1_raw1[c].rearrange("p i (m t) -> p m i t", t=PACK)[:, :, :, 2 * pair : 2 * pair + 2],
            )

        for c in range(2):
            round_w1(c, 0, nc.vector.tensor_copy)
            round_w1(c, 1, nc.scalar.copy)
        for t in range(PACK):
            cols = slice(t * P, (t + 1) * P)
            nc.vector.quantize_mx(
                out=w1_w[:, 1, cols].bitcast(FP8X4), scales=w1_s[:, 1, cols], in_=w1_bf1[t // 2][:, t % 2, :]
            )

        w4_w = held("w4_w", [P, N], U32)
        w4_s = held("w4_s", [P, N], U8)
        first_bf = held("w4_bf", [P, P * PACK], BF16)
        nc.vector.tensor_copy(
            first_bf[:].rearrange("p (c e i) -> p c i e", e=4, i=PACK),
            w4_first[:].rearrange("p i (c e) -> p c i e", e=4),
        )
        nc.vector.quantize_mx(out=w4_w[:, :P].bitcast(FP8X4), scales=w4_s[:, :P], in_=first_bf[:])
        rest_bf = held("w4_bf", [P, (N - P) * PACK], BF16)
        nc.gpsimd.tensor_scalar(
            rest_bf[:].rearrange("p (c e i) -> p c i e", e=2, i=PACK),
            w4_rest[:].rearrange("p i (c e) -> p c i e", e=2),
            1.0, 0.0, ALU.mult, ALU.add,
        )

        def pass_over_v(out, a, words, scales, first, width):
            u, inner = divmod(first, HALF)
            nc.tensor.matmul_mx(
                out=out, lhsT=words, lhsT_scale=scales,
                rhs=v_w[a][u][:, inner : inner + width].bitcast(FP8X4),
                rhs_scale=v_planes[a][:, first : first + width],
                start=(a == 0), stop=(a == PASSES - 1),
            )

        def w1_pass(w1_bank, a, t, u):
            cols = slice(t * P, (t + 1) * P)
            pass_over_v(w1_bank[:], a, w1_w[:, a, cols].bitcast(FP8X4), w1_s[:, a, cols], u * HALF, HALF)

        def w2_pass(w2_bank, a, t, u):
            words = w2_w[:, a, 2 * t * P : 2 * (t + 1) * P].bitcast(FP4X4)
            pass_over_v(w2_bank[:], a, words, w2_s[:, a, t * P : (t + 1) * P], u * HALF, HALF)

        h = [held("h%d" % u, [P, PACK, HALF], F32) for u in range(HALVES)]
        h_bf = {}
        h_w = [held("h_w%d" % u, [P, HALF], U32) for u in range(HALVES)]
        h_s = held("h_s", [P, S], U8)
        h_rows = out_1.rearrange("(p t) j -> p t j", t=PACK)
        h_codes = out_2[0].rearrange("p m i -> p (m i)").bitcast(I32)

        def square(w1_bank):
            squared = work.tile([P, HALF], F32, name="squared", bufs=PACK + 1, align_bytes=256)
            nc.scalar.activation(squared[:], w1_bank[:], ACT.Square)
            return squared

        def combine(squared, w2_bank, t, u):
            nc.vector.scalar_tensor_tensor(
                h[u][:, t, :], squared[:], gain_t[:, t : t + 1], w2_bank[:], ALU.mult, ALU.add
            )

        def store_h(u):
            nc.sync.dma_start(h_rows[:, :, u * HALF : (u + 1) * HALF], h[u][:])

        def round_h(k, parts=1):
            u, inner = divmod(k * PIECE, HALF)
            h_bf[k] = held("h_bf%d" % u, [P, PIECE * PACK], BF16)
            source = h[u][:, :, inner : inner + PIECE]
            if inner == 0:
                width = PIECE // parts
                for first in range(0, PIECE, width):
                    nc.vector.tensor_copy(
                        h_bf[k][:, first * PACK : (first + width) * PACK].rearrange("p (c e t) -> p c t e", e=4, t=PACK),
                        source[:, :, first : first + width].rearrange("p t (c e) -> p c t e", e=4),
                    )
            else:
                nc.gpsimd.tensor_scalar(
                    h_bf[k][:].rearrange("p (c e t) -> p c t e", e=2, t=PACK),
                    source.rearrange("p t (c e) -> p c t e", e=2),
                    1.0, 0.0, ALU.mult, ALU.add,
                )

        def h_piece(k):
            u, inner = divmod(k * PIECE, HALF)
            return h_w[u][:, inner : inner + PIECE].bitcast(FP8X4), h_s[:, k * PIECE : (k + 1) * PIECE]

        def quantise_h(k, parts=1):
            u, inner = divmod(k * PIECE, HALF)
            width = PIECE // parts
            for first in range(0, PIECE, width):
                nc.vector.quantize_mx(
                    out=h_w[u][:, inner + first : inner + first + width].bitcast(FP8X4),
                    scales=h_s[:, k * PIECE + first : k * PIECE + first + width],
                    in_=h_bf[k][:, first * PACK : (first + width) * PACK],
                )

        def store_codes(u):
            nc.sync.dma_start(h_codes[:, u * HALF : (u + 1) * HALF], h_w[u][:].bitcast(I32))

        def response(k, n):
            rows = slice(n * P, (n + 1) * P)
            words, scales = h_piece(k)
            q_sum = psum.tile([P, PIECE], F32, name="bank%d" % Q_BANKS[k][n])
            nc.tensor.matmul_mx(
                out=q_sum[:], lhsT=w4_w[:, rows].bitcast(FP8X4), lhsT_scale=w4_s[:, rows],
                rhs=words, rhs_scale=scales, start=True, stop=True,
            )
            magnitude = work.tile([P, PIECE], F32, name="magnitude", bufs=ROW_TILES, align_bytes=256)
            root = work.tile([P, PIECE], F32, name="root", bufs=y_tiles, align_bytes=256)
            nc.scalar.activation(magnitude[:], q_sum[:], ACT.Abs)
            nc.scalar.activation(root[:], magnitude[:], ACT.Abs_reciprocal_sqrt, bias=1.0)
            if (k, n) not in TWICE:
                inverse = work.tile([P, PIECE], F32, name="inverse", bufs=y_tiles - len(TWICE), align_bytes=256)
                nc.scalar.activation(inverse[:], root[:], ACT.Square)
                return inverse[:]
            return root[:]

        def direct(u, n):
            c_sum = bank(C_BANKS[u][n])
            for a in range(PASSES):
                scales = w3_s[:, a * N + n * P : a * N + (n + 1) * P]
                pass_over_v(c_sum[:], a, w3_w[:, a, n * P : (n + 1) * P].bitcast(FP8X4), scales, u * HALF, HALF)
            return c_sum

        def times_c(k, n, product):
            inner = k * PIECE % HALF
            c_part = sums[k * PIECE // HALF, n][:, inner : inner + PIECE]
            nc.vector.tensor_tensor(product[:], c_part, factors[k, n], ALU.mult)
            return product[:]

        def y_tile():
            return work.tile([P, PIECE], F32, name="y", bufs=y_tiles - len(TWICE), align_bytes=256)

        def store_y(k, n, y):
            nc.sync.dma_start(out_0[n * P : (n + 1) * P, k * PIECE : (k + 1) * PIECE], y)

        w1_banks = [bank(t) for t in range(PACK)]
        w2_banks = [bank(PACK + t) for t in range(PACK)]
        for t in range(PACK):
            w1_pass(w1_banks[t], 0, t, 0)
        for a in range(PASSES):
            for t in range(PACK):
                w2_pass(w2_banks[t], a, t, 0)
        for t in range(PACK):
            w1_pass(w1_banks[t], 1, t, 0)
            combine(square(w1_banks[t]), w2_banks[t], t, 0)
        for pair in (slice(0, 2), slice(2, PACK)):
            nc.sync.dma_start(h_rows[:, pair, :HALF], h[0][:, pair, :])

        def w1_squared(t):
            w1_bank = bank(t)
            for a in range(PASSES):
                w1_pass(w1_bank, a, t, 1)
            return square(w1_bank)

        def second_half(t):
            w2_bank = bank(SECOND_W2_BANKS[t])
            for a in range(PASSES):
                w2_pass(w2_bank, a, t, 1)
            combine(squares[t], w2_bank, t, 1)

        squares = [w1_squared(t) for t in range(PACK)]
        nc.vector.quantize_mx(out=w4_w[:, P:].bitcast(FP8X4), scales=w4_s[:, P:], in_=rest_bf[:])
        round_h(0, 2)
        quantise_h(0, 2)
        factors = {(0, n): response(0, n) for n in range(ROW_TILES)}
        round_h(1)
        for t in range(PACK):
            second_half(t)
        store_h(1)
        quantise_h(1)
        store_codes(0)
        for n in range(ROW_TILES):
            factors[1, n] = response(1, n)
        sums = {(0, n): direct(0, n) for n in range(ROW_TILES)}
        round_h(2, 2)
        quantise_h(2, 2)
        for n in range(ROW_TILES):
            factors[2, n] = response(2, n)
        round_h(3)
        pair = held("pair", [P, 2, PIECE], F32)
        for n in range(ROW_TILES - 1):
            times_c(0, n, pair[:, n, :])
        nc.sync.dma_start(out_0[: 2 * P, :PIECE].rearrange("(n p) j -> p n j", p=P), pair[:])
        once = {}

        def first_product(k, n):
            once[k, n] = times_c(k, n, held("once%d%d" % (k, n), [P, PIECE], F32))

        def second_product(k, n, y, engine=nc.vector):
            engine.tensor_tensor(y, once[k, n], factors[k, n], ALU.mult)
            store_y(k, n, y)

        for k, n in TWICE[: 1 + ROW_TILES]:
            first_product(k, n)
        quantise_h(3)
        store_codes(1)
        for n in range(ROW_TILES):
            factors[3, n] = response(3, n)
        for s in range(4):
            nc.sync.dma_start(out_3[0, s:16:4, :].bitcast(I32), h_s[s:P:32, :].bitcast(I32))
        early_y = held("h_bf%d" % (HALVES - 1), [P, ROW_TILES, PIECE], F32)
        second_product(0, 2, early_y[:, 0, :])
        for n in range(2):
            nc.vector.tensor_tensor(early_y[:, 1 + n, :], once[1, n], factors[1, n], ALU.mult)
        nc.sync.dma_start(out_0[: 2 * P, PIECE : 2 * PIECE].rearrange("(n p) j -> p n j", p=P), early_y[:, 1:, :])
        second_product(1, 2, held("once11", [P, PIECE], F32)[:], nc.gpsimd)
        for n in range(ROW_TILES):
            sums[1, n] = direct(1, n)
        late_tiles = TWICE[1 + ROW_TILES :]
        for k, n in late_tiles:
            first_product(k, n)
        late_y = held("once12", [P, len(late_tiles), PIECE], F32)
        for place, (k, n) in enumerate(late_tiles):
            second_product(k, n, late_y[:, place, :])
        for n in range(1, ROW_TILES):
            store_y(3, n, times_c(3, n, y_tile()))
